import numpy as np, ml_dtypes
CORES = [10,34,74,98]
N = 4
BF = ml_dtypes.bfloat16
def gentries(a):
    return np.ascontiguousarray(a.reshape(8, 16, -1).transpose(0, 2, 1)).reshape(8, -1)
def gtable(e):
    e = np.asarray(e); return np.ascontiguousarray(e.reshape(8, -1, 16).transpose(0, 2, 1)).reshape(128, -1).astype(np.int32)
U, D, RO, W = 1024, 4, 4, 4096
def parts(rng):
    a = (rng.integers(32, 257, (N, 8, 1, U)) * rng.random((N, 8, 16, U))).astype(np.int64)
    s = rng.integers(0, W, (N, 8, D, U))
    w = np.where(rng.random((N, 8, 1, U)) < 0.5, rng.integers(-1, 2, s.shape), rng.integers(-3, 4, s.shape))
    return a, s, w, rng.integers(-300, 501, (N, 8, U))
def pack(a, s, w, b):
    return {"a0": np.ascontiguousarray(a.reshape(N, 128, U)).astype(np.float32).astype(BF), "sr": np.stack([gtable(x.reshape(8, D * U)) for x in s]),
            "wt": np.ascontiguousarray(w.reshape(N, 8, D * U)).astype(np.int32), "bs": np.ascontiguousarray(b).astype(np.int32)}
def setup_inputs(rng):
    return pack(*parts(rng))
def setup_inputs_ties(rng):
    a, s, w, b = parts(rng); a[..., 1::2] = a[..., ::2]
    m = rng.integers(0, 4, (N, 8, 1, U)); pick = rng.integers(0, 2, s.shape); x = s[:, :, :1]; y = s[:, :, 1:2]
    s = np.where(m == 0, x, np.where(m == 1, x ^ pick, np.where(m == 2, np.where(pick == 1, x, y), s)))
    w = np.where(m == 3, -np.abs(w), w); b = np.where(m[:, :, 0] == 3, -np.abs(b) - 1, np.abs(b))
    for v in (s, w, b): v[:, 4:, ..., 1::2] = v[:, 4:, ..., ::2]
    return pack(a, s, w, b)
def setup_inputs_ends(rng):
    a, s, w, b = parts(rng); own = np.arange(N).reshape(N, 1, 1) * U
    s[:, 0] = rng.choice(np.concatenate([np.arange(N) * U, np.arange(N) * U + U - 1]), (N, D, U))
    s[:, 1] = rng.choice(np.array([0, W - 1]), (N, D, U))
    s[:, 2] = own + rng.integers(0, U, (N, D, U))
    s[:, 3] = (own + U + rng.integers(0, W - U, (N, D, U))) & (W - 1)
    s[:, 4] = int(rng.integers(0, N)) * U + rng.integers(0, U, (N, D, U))
    s[:, 4, 0] = s[:, 4, 0] // U * U + np.arange(U)
    s[:, 5] = own + np.arange(U)
    s[:, 6] = np.argsort(rng.random((N, W)), axis=-1)[:, :D * U].reshape(N, D, U)
    return pack(a, s, w, b)
def setup_inputs_full(rng):
    a, s, w, b = parts(rng)
    a[:, 0] = rng.integers(254, 256, (N, 16, U)); a[:, 0] = np.where(rng.random((N, 1, U)) < 0.5, 255, a[:, 0]); a[:, 0, :, 0] = 255
    s[0, 0, :, 0] = 0; w[:, 0] = rng.integers(1, 4, (N, D, U)); b[:, 0] = 1000
    w[:, 1] = -3; b[:, 1] = -1000
    w[:, 2] = 0; b[:, 2] = rng.integers(240, 256, (N, U))
    w[:, 3] = 0; b[:, 3] = rng.choice(np.array([-1, 0, 1, 254, 255, 256]), (N, U))
    a[:, 4] = 255 * rng.integers(0, 2, (N, 16, U)); w[:, 4] = rng.choice(np.array([-3, 3]), (N, D, U)); b[:, 4] = rng.choice(np.array([-1000, 0, 1000]), (N, U))
    o = rng.permutation(16); x = int(rng.integers(200, 255)); h1 = np.zeros(16, np.int64)
    h1[o[0]] = x; h1[o[1]] = x + 1; h1[o[2:]] = 2 * rng.integers(95, 128, 14)
    h2 = h1.copy(); h2[o[0]] = x + 1; h2[o[1]] = x
    a[:, 5] = np.where(rng.integers(0, 2, (N, 1, U)) == 1, h1[:, None], h2[:, None])
    w[:, 5] = np.where(np.arange(D)[:, None] == rng.integers(0, D, (N, 1, U)), 1, 0); b[:, 5] = 0
    a[:, 6:] = rng.integers(0, 4, (N, 2, 16, U)) * (rng.random((N, 2, 16, U)) < 0.3)
    w[:, 6:] = rng.integers(-1, 2, (N, 2, D, U)); b[:, 6:] = rng.integers(-4, 9, (N, 2, U))
    return pack(a, s, w, b)
def setup_inputs_crowd(rng):
    a, s, w, b = parts(rng); a = np.maximum(a, 1); q = int(rng.integers(0, N))
    s = q * U + rng.integers(0, U, s.shape)
    live = [1, 3, 4, 5, 7]
    w[:, live] = rng.integers(1, 4, (N, 5, D, U)); b[:, live] = rng.integers(0, 101, (N, 5, U))
    w[:, 0:3:2] = -rng.integers(0, 4, (N, 2, D, U)); b[:, 0:3:2] = -1000
    u = q * U + np.arange(U); cand = u[(((20 * u) & (W - 1)) // U == q) & ((u & 1) == 1)]
    s[:, 1] = rng.choice(cand, (N, 1, 1)); s[:, 7] = rng.choice(cand, (N, 1, 1))
    for g, t in ((3, 1), (4, 2), (5, D - 1)):
        z = int(rng.integers(0, U)); a[q, g, :, z] = 0
        s[:, g] = q * U + ((z + 1 + rng.integers(0, U - 1, (N, D, U))) & (U - 1)); s[:, g, t] = q * U + z
    return pack(a, s, w, b)
def setup_inputs_spread(rng):
    a, s, w, b = parts(rng)
    a = np.minimum((np.exp2(8 * rng.random((N, 8, 1, U))) * rng.random(a.shape)).astype(np.int64) + 1, 255) * (rng.random((N, 8, 1, U)) > 0.0625)
    s = np.minimum((W * rng.random(s.shape) ** rng.integers(1, 5, (N, 8, 1, 1))).astype(np.int64), W - 1); s[:, 1::2] = W - 1 - s[:, 1::2]
    w = rng.integers(-3, 4, s.shape); b = rng.integers(-1000, 1001, b.shape)
    b[:, ::3] = (np.exp2(9.9 * rng.random((N, 3, U))) * rng.choice(np.array([-1, 1]), (N, 3, U))).astype(np.int64)
    return pack(a, s, w, b)
def check_inputs(d):
    bad = []; x = np.asarray(d["a0"]).astype(np.float32)
    if not np.all((x >= 0) & (x <= 255) & (x == np.floor(x))): bad.append("whole numbers from 0 to 255 in a0")
    for k, lo, hi in (("sr", 0, W - 1), ("wt", -3, 3), ("bs", -1000, 1000)):
        if np.min(d[k]) < lo or np.max(d[k]) > hi: bad.append("range of " + k)
    return bad
def reference(a0, sr, wt, bs):
    a = a0.astype(np.float32).astype(np.int64).reshape(N, 8, 16, U)
    s = np.stack([gentries(x) for x in sr]).astype(np.int64).reshape(N, 8, D, U)
    w = wt.astype(np.int64).reshape(N, 8, 1, D, U); b = bs.astype(np.int64).reshape(N, 8, 1, U)
    for rnd in range(RO):
        every = np.ascontiguousarray(a.transpose(1, 2, 0, 3)).reshape(8, 16, W)
        na, ns = [], []
        for r in range(N):
            p = np.take_along_axis(every, s[r].reshape(8, 1, D * U), 2).reshape(8, 16, D, U)
            v = np.minimum(np.maximum(b[r] + np.add.reduce(w[r] * p, axis=2), 0), 255)
            c = np.add.reduce(p * v[:, :, None, :], axis=1)
            best = np.argmax(c, axis=1)[:, None, :]; worst = np.argmin(c, axis=1)[:, None, :]
            top = np.roll(np.take_along_axis(c, best, 1), -1, axis=0)
            new = (13 * np.take_along_axis(s[r], best, 1) + 7 * np.take_along_axis(s[r], worst, 1) + top) & (W - 1)
            na.append(v); ns.append(np.where(np.arange(D)[None, :, None] == worst, new, s[r]))
        a = np.stack(na); s = np.stack(ns)
    return {"ya": a.reshape(N, 128, U).astype(np.float32).astype(BF), "ys": np.stack([gtable(x.reshape(8, D * U)) for x in s]).astype(np.float32)}

@@ -1,0 +1,419 @@
+from concourse.bass import DstId, RemoteDMATransfer
+from concourse.mybir import AluOpType as OP, ActivationFunctionType as AF
+
+U, RO = 1024, 4
+PIECES = [(0, 256, 0), (256, 512, 1), (512, 1024, None)]
+SB = (0, 1)
+PS = (2, 3, 4, 5, 6, 7)
+ORDER = ("Y1' L0' B0 B1 e1' R1' G2 D0 G3 Z1' F0 O1' G4 F1 X0 L1' W2 K0 X1 W3 X2 G5 G6 X3 W4 K1 C0 W5 X4 G7 A0 G1 W6 X6 M0024 W7 X5 X7 "
+         "M0124 G0 M0224 D1 C1 A1 M0002 M0102 S00 M0324 S01 M0202 M0302 S02 M1004 M1104 S03 T0 M1204 N0 S10 S11 e0 M1304 S12 Y0 S13 "
+         "R0 T1 Z0 N1 O0").split()
+
+SCRATCH = {}
+for _n in ("W0", "W1", "W2"):
+    SCRATCH[_n] = ("psum", [128, 1024], "bfloat16")
+for _n in ("X0", "X1", "K0", "K1", "DD"):
+    SCRATCH[_n] = ("psum", [128, 512], "float32")
+for _n, _w, _d in (
+        ("win0", 4096, "bfloat16"), ("win1", 4096, "bfloat16"), ("win2", 4096, "bfloat16"), ("win3", 4096, "bfloat16"),
+        ("vo", 1024, "bfloat16"), ("p", 4096, "bfloat16"), ("wp", 4096, "float16"), ("pv", 4096, "float32"),
+        ("wsb", 4096, "bfloat16"), ("wi", 1024, "int32"), ("wb", 1024, "bfloat16"), ("bi", 512, "int32"), ("bh", 512, "float16"),
+        ("lraw", 256, "int32"), ("off", 256, "uint16"), ("lf", 256, "float32"), ("ly", 256, "float32"), ("yb", 1024, "float32"),
+        ("z1", 128, "bfloat16"), ("z2", 128, "bfloat16"), ("z3", 128, "bfloat16"), ("z4", 16, "bfloat16"), ("ge", 16, "float32"),
+        ("fs", 512, "bfloat16"), ("fh", 256, "float16"), ("ih", 128, "float16"), ("ib", 128, "bfloat16"),
+        ("dm", 256, "float32"), ("bm", 160, "float32"), ("tmp", 128, "bfloat16"), ("tm2", 128, "bfloat16"),
+        ("bk", 32, "float32"), ("rst", 272, "float32"), ("ones", 128, "bfloat16"), ("koff", 272, "bfloat16"), ("c255", 4, "float32")):
+    SCRATCH[_n] = ("sbuf", [128, _w], _d)
+for _h in range(2):
+    for _n, _w, _d in (("mx", 272, "float32"), ("ne", 256, "float32"), ("yy", 256, "float32"), ("ew", 128, "float32"),
+                       ("sk", 128, "float32"), ("tt", 128, "float32"), ("aa", 64, "float32"), ("ai", 64, "int32")):
+        SCRATCH["%s%d" % (_n, _h)] = ("sbuf", [128, _w], _d)
+
+SEMAPHORES = ["V", "S", "P", "G", "la0", "la1", "lw", "lb", "ls", "st", "sent", "arr0", "arr1", "arr2", "arr3"]
+
+
+def bits(engines):
+    return sum(1 << e for e in engines)
+
+
+def dst_id(c, topo):
+    return DstId(rid=topo.addr(c)[0], pnc=topo.addr(c)[1])
+
+
+def helpers_of(core, cores, topo):
+    peers = [c for c in cores if c != core]
+    able = [c for c in topo.cores_of(core) if c != core and all(topo.may_write(c, d) for d in peers)]
+    return sorted(able, key=lambda c: topo.die(c) == topo.die(core))
+
+
+def fan_out(g, T, topo, src, rank, ap, sem):
+    n = len(T.cores)
+    dsts = [T.cores[(rank + k) % n] for k in range(1, n)]
+    eng = topo.engines(src, dsts[0])
+    g.remote_dma_fused([RemoteDMATransfer(dst_ids=[dst_id(d, topo) for d in dsts], dma_engine_mask=bits(eng), remote_sem=sem,
+                                          src=ap, dsts=[ap] * len(dsts))], local_sem=T.sem.sent)
+    return len(eng)
+
+
+def hand_engines(core, cores, topo, r, h):
+    eng = topo.engines(core, helpers_of(core, cores, topo)[0])
+    vias = [via for c0, c1, via in PIECES if c0 // 512 == h]
+    if r == 0 or None in vias:
+        far = topo.engines(core, [c for c in cores if c != core][0])
+        eng = [e for e in eng if e not in far]
+    vias = [via for via in vias if via is not None]
+    n = len(eng) // len(vias)
+    return {via: eng[i * n:i * n + n] for i, via in enumerate(vias)}
+
+
+def helper_program(g, core, owner, k, T, topo):
+    rank = T.rank_of(owner)
+    sent = 0
+    for r in range(RO):
+        for c0, c1, via in PIECES:
+            if via == k:
+                g.wait_ge(T.sem["arr%d" % r], len(hand_engines(owner, T.cores, topo, r, c0 // 512)[k]))
+                sent += fan_out(g, T, topo, core, rank, T["win%d" % r][:, rank * U + c0:rank * U + c1], T.sem["arr%d" % r])
+    if sent:
+        g.wait_ge(T.sem.sent, sent)
+
+
+def rank_program(g, core, T, topo):
+    rank = T.rank_of(core)
+    if rank is None:
+        for c in T.cores:
+            hs = helpers_of(c, T.cores, topo)
+            if core in hs:
+                helper_program(g, core, c, hs.index(core), T, topo)
+        return
+    cores = T.cores
+    R = rank * U
+    helpers = helpers_of(core, cores, topo)
+    n_arr = 0
+    for c in cores:
+        if c != core:
+            for c0, c1, via in PIECES:
+                n_arr += len(topo.engines(c if via is None else helpers_of(c, cores, topo)[via], core))
+
+    Q = {"V": g.vector, "S": g.scalar, "P": g.tensor, "G": g, "Y": g.sync}
+    cnt = {"V": 0, "S": 0, "P": 0, "G": 0}
+    clock = {q: {} for q in Q}
+    snap = {}
+    lastw, readers, bankuse = {}, {}, {}
+
+    def need(q, toks):
+        best = {}
+        for s, n in toks:
+            if clock[q].get(s, 0) < n and best.get(s, 0) < n:
+                best[s] = n
+        for s, n in sorted(best.items(), key=lambda x: -len(snap.get(x, {}))):
+            if clock[q].get(s, 0) >= n:
+                continue
+            Q[q].wait_ge(T.sem[s], n)
+            clock[q][s] = n
+            for s2, n2 in snap.get((s, n), {}).items():
+                if clock[q].get(s2, 0) < n2:
+                    clock[q][s2] = n2
+
+    def deps(q, rd, wr, banks):
+        toks = [lastw[k] for k in list(rd) + list(wr) if k in lastw]
+        for k in wr:
+            toks.extend(readers.get(k, []))
+        if q == "P":
+            toks = [t for t in toks if t[0] != "P"]
+        for b in banks:
+            toks.extend(t for e, t in bankuse.get(b, {}).items() if e != q)
+        return toks
+
+    def note(q, tok, rd, wr, banks):
+        for k in rd:
+            readers.setdefault(k, []).append(tok)
+        for k in wr:
+            lastw[k] = tok
+            readers[k] = []
+        for b in banks:
+            bankuse.setdefault(b, {})[q] = tok
+
+    def op(q, fn, rd=(), wr=(), banks=()):
+        need(q, deps(q, rd, wr, banks))
+        cnt[q] += 1
+        tok = (q, cnt[q])
+        fn().then_inc(T.sem[q], 1)
+        snap[tok] = dict(clock[q])
+        note(q, tok, rd, wr, banks)
+
+    def dma(q, out, in_, sem, total, rd=(), wr=()):
+        need(q, deps(q, rd, wr, ()))
+        Q[q].dma_start(out, in_).then_inc(T.sem[sem], 16)
+        note(q, (sem, total), rd, wr, ())
+
+    V, S, P = g.vector, g.scalar, g.tensor
+    sent = [0]
+
+    def send(r, h):
+        need("G", [lastw["v%d%d" % (r, h)]])
+        sem = T.sem["arr%d" % r]
+        hand = []
+        for c0, c1, via in PIECES:
+            if c0 // 512 == h and via is not None:
+                ap = T["win%d" % r][:, R + c0:R + c1]
+                eng = hand_engines(core, cores, topo, r, h)[via]
+                hand.append(RemoteDMATransfer(dst_ids=[dst_id(helpers[via], topo)], dma_engine_mask=bits(eng), remote_sem=sem, src=ap, dst=ap))
+                sent[0] += len(eng)
+        if hand:
+            g.remote_dma_fused(hand, local_sem=T.sem.sent)
+        for c0, c1, via in PIECES:
+            if c0 // 512 == h and via is None:
+                sent[0] += fan_out(g, T, topo, core, rank, T["win%d" % r][:, R + c0:R + c1], sem)
+
+    dma("Y", T.win0[:, R:R + 512], T.a0[:, 0:512], "la0", 16, wr=["v00"])
+    dma("S", T.win0[:, R + 512:R + U], T.a0[:, 512:U], "la1", 16, wr=["v01"])
+    dma("Y", T.wi[0:32, :], T.wt[:, :], "lw", 16, wr=["wi"])
+    dma("S", T.bi[0:16, :], T.bs[:, :], "lb", 16, wr=["bi"])
+    for a in range(4):
+        dma("YS"[a % 2], T.lraw[:, 64 * a:64 * a + 64], T.sr[a::4, :], "ls", 64, wr=["lraw%d" % a])
+
+    imp = {"allow_small_or_imprecise_dtypes": True}
+    op("G", lambda: g.iota(T.z2[0:32, :], [[-4, 8], [0, 16]], 0, 1, **imp), wr=["z2"])
+    op("G", lambda: g.iota(T.z1[:, :], [[1, 128]], 0, -1, **imp), wr=["z1"])
+    op("G", lambda: g.iota(T.z3[0:16, :], [[-2, 8], [0, 16]], 0, 1, **imp), wr=["z3"])
+    op("G", lambda: g.iota(T.z4[:, 0:16], [[-16, 16]], 0, 1, **imp), wr=["z4"])
+    send(0, 0)
+    send(0, 1)
+    for r in range(RO):
+        lastw["arr%d" % r] = ("arr%d" % r, n_arr)
+
+    def ts(out, in0, s1, op0, rd, wr, s2=None, op1=None, banks=()):
+        if op1 is None:
+            op("V", lambda: V.tensor_scalar(out, in0, s1, None, op0), rd, wr, banks)
+        else:
+            op("V", lambda: V.tensor_scalar(out, in0, s1, s2, op0, op1), rd, wr, banks)
+
+    def tt(out, in0, in1, o, rd, wr, banks=()):
+        op("V", lambda: V.tensor_tensor(out, in0, in1, o), rd, wr, banks)
+
+    def vcopy(out, in_, rd, wr, banks=()):
+        op("V", lambda: V.tensor_copy(out, in_), rd, wr, banks)
+
+    def act(out, in_, rd, wr, banks=(), f=AF.Copy, bias=0.0, scale=1.0):
+        op("S", lambda: S.activation(out, in_, f, bias, scale), rd, wr, banks)
+
+    def mm(out, lhsT, rhs, start, stop, rd, wr, banks):
+        op("P", lambda: P.matmul(out, lhsT, rhs, start, stop), rd, wr, banks)
+
+    def four(name):
+        return [name + str(i) for i in range(4)]
+
+    op("V", lambda: V.memset(T.rst[:, :], 0.0), wr=["rst"])
+    op("V", lambda: V.memset(T.ones[0:1, :], 1.0), wr=["ones"])
+    op("V", lambda: V.memset(T.c255[:, :], 255.0), wr=["c255"])
+    for s in range(4):
+        op("V", lambda: V.memset(T.koff[0:1, s::4], (1.5 - s) / 4), wr=["koff%d" % s])
+    op("V", lambda: V.memset(T.rst[:, 0::4], -4194304.0), wr=["rst"])
+    for s in range(4):
+        ts(T.fs[0:32, 128 * s:128 * s + 128], T.z2[0:32, :], float(s), OP.is_equal, ["z2"], ["fs%d" % s])
+    ident = T.bm[:, 32:160]
+    ts(T.ib[:, :], T.z1[:, :], 0.0, OP.is_equal, ["z1"], ["ib"])
+    ts(T.tmp[:, :], T.z1[:, :], 1.0, OP.is_equal, ["z1"], ["tmp"])
+    ts(T.ih[:, :], T.z1[:, :], 0.0, OP.is_equal, ["z1"], ["ih"])
+    tt(T.tm2[:, :], T.tmp[:, :], T.ib[:, :], OP.subtract, ["tmp", "ib"], ["tm2"])
+    for h in range(2):
+        ts(T.fh[0:16, 128 * h:128 * h + 128], T.z3[0:16, :], float(h), OP.is_equal, ["z3"], ["fh%d" % h])
+    ts(T.ge[:, :], T.z4[:, :], 0.0, OP.is_ge, ["z4"], ["ge"])
+    act(ident, T.ib[:, :], ["ib"], ["ident"])
+    act(T.bm[:, 0:32], T.ib[:, 3::4], ["ib"], ["base"], scale=20.0)
+    act(T.dm[:, 0:128], T.tm2[:, :], ["tm2"], ["dm0"], scale=7.0)
+    act(T.dm[:, 128:256], T.tm2[:, :], ["tm2"], ["dm1"], scale=13.0)
+    tt(T.bk[:, 0:8], T.ge[:, 1:9], T.ge[:, 0:8], OP.subtract, ["ge"], ["bk0"])
+    tt(T.bk[:, 8:16], T.ge[:, 0:8], T.ge[:, 1:9], OP.subtract, ["ge"], ["bk1"])
+    tt(T.bk[:, 16:17], T.ge[:, 0:1], T.ge[:, 1:2], OP.subtract, ["ge"], ["bk2"])
+    for h in range(2):
+        vcopy(T.wb[0:32, 512 * h:512 * h + 512], T.wi[0:32, 512 * h:512 * h + 512], ["wi"], ["wb%d" % h])
+
+    def wcols(b):
+        c = 512 * (SB + PS).index(b)
+        return slice(c, c + 512)
+
+    def weights(b, bank, copy):
+        h, a = divmod(b, 4)
+        for s in range(4):
+            mm(T[bank][:, s::4], T.fs[0:32, 128 * s:128 * s + 128], T.wb[0:32, 512 * h + a:512 * h + 512:4], True, True,
+               ["fs%d" % s, "wb%d" % h], ["stg%s%d" % (bank, s)], [bank])
+        return lambda: copy(T.wsb[:, wcols(b)], T[bank][:, :], four("stg" + bank), ["ws%d" % b], [bank])
+
+    def weights_to_psum(k):
+        vcopy(T["W%d" % k][:, :], T.wsb[:, 1024 * (k + 1):1024 * (k + 2)], ["ws%d" % b for b in PS[2 * k:2 * k + 2]], ["W%d" % k], ["W%d" % k])
+
+    weights(PS[0], "X0", act)()
+    weights(PS[1], "X1", act)()
+    later = weights(SB[0], "K0", vcopy)
+    for b, bank in ((SB[1], "K1"), (PS[2], "DD"), (PS[3], "X0"), (PS[4], "X1"), (PS[5], "K1")):
+        weights(b, bank, act)()
+    for a in range(4):
+        for h in range(2):
+            vcopy(T.off[:, 128 * h + 32 * a:128 * h + 32 * a + 32], T.lraw[:, 64 * a + 32 * h:64 * a + 32 * h + 32],
+                  ["lraw%d" % a], ["offi%d%d" % (h, a)])
+    later()
+    weights_to_psum(0)
+    for a in range(4):
+        vcopy(T.bh[0:16, 128 * a:128 * a + 128], T.bi[0:16, a::4], ["bi"], ["bh%d" % a])
+    for h in range(2):
+        vcopy(T.lf[:, 128 * h:128 * h + 128], T.off[:, 128 * h:128 * h + 128], four("offi%d" % h), ["lf%d" % h, "off%d" % h])
+    weights_to_psum(1)
+    weights_to_psum(2)
+
+    def cols(b):
+        return slice(512 * b, 512 * b + 512)
+
+    def gathered(r, b):
+        return T["win%d" % r][:, 0:4096].indirect(T.off[:, 32 * b:32 * b + 32])
+
+    def win_keys(r, b):
+        return ["arr%d" % r, "v%d0" % r, "v%d1" % r, "off%d" % (b // 4)]
+
+    def gather(r, b):
+        op("S", lambda: S.activation(T.p[:, cols(b)], gathered(r, b), AF.Copy), win_keys(r, b), ["p%d" % b])
+
+    def gather_weigh(r, b):
+        tt(T.wp[:, cols(b)], gathered(r, b), T.wsb[:, wcols(b)], OP.mult, win_keys(r, b) + ["ws%d" % b], ["wp%d" % b])
+
+    def weigh(r, b):
+        if b in SB:
+            tt(T.wp[:, cols(b)], T.p[:, cols(b)], T.wsb[:, wcols(b)], OP.mult, ["p%d" % b, "ws%d" % b], ["wp%d" % b])
+        else:
+            k, half = divmod(PS.index(b), 2)
+            tt(T.wp[:, cols(b)], T.p[:, cols(b)], T["W%d" % k][:, 512 * half:512 * half + 512], OP.mult,
+               ["p%d" % b, "W%d" % k], ["wp%d" % b], ["W%d" % k])
+
+    def bias(r, h):
+        mm(T["X%d" % h][:, :], T.fh[0:16, 128 * h:128 * h + 128], T.bh[0:16, :], True, False,
+           ["fh%d" % h] + four("bh"), ["xb%d" % h, "xv%d" % h], ["X%d" % h])
+
+    done = {}
+
+    def closes(key):
+        done[key] = done.get(key, 0) + 1
+        return done[key] == 4
+
+    def wsum(r, b):
+        h, a = divmod(b, 4)
+        last = closes(("x", r, h))
+        for s in range(4):
+            mm(T["X%d" % h][:, 128 * a:128 * a + 128], T.ih[:, :], T.wp[:, 512 * b + s:512 * b + 512:4], False, last and s == 3,
+               ["ih", "wp%d" % b, "xb%d" % h], ["x%d%d" % (h, a)], ["X%d" % h])
+
+    def diffs(r, h):
+        mm(T.DD[:, 256 * h:256 * h + 256], T.lf[:, 128 * h:128 * h + 128], T.dm[:, :], True, True,
+           ["lf%d" % h, "dm0", "dm1"], ["d%d" % h], ["DD"])
+
+    def keys_open(r, h):
+        K = T["K%d" % h]
+        mm(K[:, 272:432], T.lf[:, 128 * h:128 * h + 128], T.bm[:, :], True, True, ["lf%d" % h, "ident", "base"], ["ks%d" % h], ["K%d" % h])
+        mm(K[:, 0:272], T.ones[0:1, :], T.koff[0:1, :], True, False, ["ones"] + four("koff"), ["kb%d" % h] + four("k%d" % h), ["K%d" % h])
+
+    def new_act(r, h):
+        return (T.vo, 512 * h) if r == RO - 1 else (T["win%d" % (r + 1)], R + 512 * h)
+
+    def pass_on(r, h):
+        if r == RO - 1:
+            dma("Y", T.ya[:, 512 * h:512 * h + 512], T.vo[:, 512 * h:512 * h + 512], "st", 96, rd=["v%d%d" % (r + 1, h)])
+        else:
+            send(r + 1, h)
+
+    def clamp(r, h):
+        buf, c0 = new_act(r, h)
+        key = "v%d%d" % (r + 1, h)
+        for a in range(4):
+            ts(buf[:, c0 + a:c0 + 512:4], T["X%d" % h][:, 128 * a:128 * a + 128], 0.0, OP.max, four("x%d" % h),
+               [key] if a == 3 else [key + "_%d" % a], 255.0, OP.min, ["X%d" % h])
+        pass_on(r, h)
+
+    def clamp_scalar(r, h):
+        buf, c0 = new_act(r, h)
+        key = "v%d%d" % (r + 1, h)
+        act(T.yb[:, 512 * h:512 * h + 512], T["X%d" % h][:, :], four("x%d" % h) + ["c255"], ["yb%d" % h], ["X%d" % h], AF.Relu, T.c255[:, 0:1], -1.0)
+        for a in range(4):
+            act(buf[:, c0 + a:c0 + 512:4], T.yb[:, 512 * h + 128 * a:512 * h + 128 * a + 128], ["yb%d" % h],
+                [key] if a == 3 else [key + "_%d" % a], (), AF.Relu, T.c255[:, 0:1], -1.0)
+        pass_on(r, h)
+
+    def act_to_psum(r, h):
+        buf, c0 = new_act(r, h)
+        for a in range(4):
+            mm(T["X%d" % h][:, 128 * a:128 * a + 128], T.ib[:, :], buf[:, c0 + a:c0 + 512:4], True, True,
+               ["ib", "v%d%d" % (r + 1, h)], ["xv%d" % h], ["X%d" % h])
+
+    def prod(r, h, s, a0, a1):
+        c = 2048 * h + 512 * s
+        tt(T.pv[:, c + 128 * a0:c + 128 * a1], T.p[:, 2048 * h + 512 * a0 + s:2048 * h + 512 * a1:4], T["X%d" % h][:, 128 * a0:128 * a1],
+           OP.mult, ["p%d" % (4 * h + a) for a in range(a0, a1)] + ["xv%d" % h], ["pv%d%d%d" % (h, s, a) for a in range(a0, a1)], ["X%d" % h])
+
+    def score(r, h, s):
+        c = 2048 * h + 512 * s
+        last = closes(("k", r, h))
+        for cc in range(4):
+            mm(T["K%d" % h][:, 4 * cc + s:272:16], T.pv[:, c + cc:c + 512:4], T.bk[:, 0:17], False, last and cc == 3,
+               four("pv%d%d" % (h, s)) + ["bk0", "bk1", "bk2", "kb%d" % h], ["k%d%d" % (h, s)], ["K%d" % h])
+
+    def scan1(r, h):
+        op("V", lambda: V.tensor_tensor_scan(T["mx%d" % h][:, :], T.rst[:, :], T["K%d" % h][:, 0:272], 0.0, OP.add, OP.max),
+           ["rst"] + four("k%d" % h), ["mx%d" % h], ["K%d" % h])
+
+    def flags(r, h):
+        for s in range(4):
+            tt(T["ne%d" % h][:, s::4], T["K%d" % h][:, s:256:4], T["mx%d" % h][:, 3:256:4], OP.not_equal,
+               ["k%d%d" % (h, s), "mx%d" % h], ["ne%d%d" % (h, s)], ["K%d" % h])
+
+    def worst_scalar(r, h):
+        act(T["ew%d" % h][:, :], T["ne%d" % h][:, 0:128], four("ne%d" % h), ["ew%d" % h], (), AF.Identity, 1.0, -1.0)
+
+    def worst(r, h):
+        ts(T["ew%d" % h][:, :], T["ne%d" % h][:, 0:128], -1.0, OP.mult, four("ne%d" % h), ["ew%d" % h], 1.0, OP.add)
+
+    def scan2(r, h):
+        op("V", lambda: V.tensor_tensor_scan(T["yy%d" % h][:, :], T.DD[:, 256 * h:256 * h + 256], T["ne%d" % h][:, :], 0.0, OP.add, OP.mult),
+           ["d%d" % h] + four("ne%d" % h), ["yy%d" % h], ["DD"])
+
+    def new_source(r, h):
+        K, aa, ai, yy = T["K%d" % h], T["aa%d" % h], T["ai%d" % h], T["yy%d" % h]
+        tt(aa[:, 32:64], T["mx%d" % h][:, 147:272:4], K[:, 272:304], OP.add, ["mx%d" % h, "ks%d" % h], ["a2%d" % h], ["K%d" % h])
+        tt(aa[:, 0:32], yy[:, 3:128:4], yy[:, 131:256:4], OP.add, ["yy%d" % h], ["a1%d" % h])
+        tt(T["sk%d" % h][:, :], T["ne%d" % h][:, 0:128], K[:, 304:432], OP.mult, four("ne%d" % h) + ["ks%d" % h], ["sk%d" % h], ["K%d" % h])
+        tt(ai[:, 0:32], aa[:, 0:32], aa[:, 32:64], OP.add, ["a1%d" % h, "a2%d" % h], ["a3%d" % h])
+        mm(K[:, 304:432], T["sk%d" % h][:, :], ident, True, False, ["sk%d" % h, "ident"], ["ks%d" % h], ["K%d" % h])
+
+    def rewire(r, h):
+        K, ai = T["K%d" % h], T["ai%d" % h]
+        ts(ai[:, 32:64], ai[:, 0:32], 4095, OP.bitwise_and, ["a3%d" % h], ["a4%d" % h])
+        for s in range(4):
+            tt(T["tt%d" % h][:, s::4], T["ew%d" % h][:, s::4], ai[:, 32:64], OP.mult, ["ew%d" % h, "a4%d" % h], ["tt%d%d" % (h, s)])
+        mm(K[:, 304:432], T["tt%d" % h][:, :], ident, False, True, four("tt%d" % h) + ["ident"], ["ks%d" % h], ["K%d" % h])
+
+    def sources_out(h, copy):
+        for a in range(4):
+            copy(T.ly[:, 64 * a + 32 * h:64 * a + 32 * h + 32], T["K%d" % h][:, 304 + 32 * a:336 + 32 * a], ["ks%d" % h],
+                 ["ly%d%d" % (h, a)], ["K%d" % h])
+
+    def offsets(r, h):
+        if r < RO - 1:
+            vcopy(T.off[:, 128 * h:128 * h + 128], T["K%d" % h][:, 304:432], ["ks%d" % h], ["off%d" % h], ["K%d" % h])
+        elif h == 1:
+            sources_out(h, vcopy)
+
+    def sources(r, h):
+        if r < RO - 1:
+            act(T.lf[:, 128 * h:128 * h + 128], T["K%d" % h][:, 304:432], ["ks%d" % h], ["lf%d" % h], ["K%d" % h])
+        elif h == 0:
+            sources_out(h, act)
+
+    STEP = {"B": bias, "D": diffs, "K": keys_open, "F": gather_weigh, "G": gather, "W": weigh, "X": wsum, "C": clamp, "c": clamp_scalar,
+            "A": act_to_psum, "M": prod, "S": score, "T": scan1, "N": flags, "e": worst_scalar, "E": worst, "Y": scan2,
+            "R": new_source, "Z": rewire, "O": offsets, "L": sources}
+    for r in range(RO + 1):
+        for step in ORDER:
+            rr = r - step.count("'")
+            if 0 <= rr < RO:
+                STEP[step[0]](rr, *[int(c) for c in step[1:].strip("'")])
+    for a in range(4):
+        dma("YS"[a % 2], T.ys[a::4, :], T.ly[:, 64 * a:64 * a + 64], "st", 96, rd=["ly0%d" % a, "ly1%d" % a])
+    need("G", [("V", cnt["V"]), ("S", cnt["S"]), ("P", cnt["P"]), ("G", cnt["G"]), ("sent", sent[0]), ("st", 96)])

@@ -2,34 +2,42 @@ from concourse.bass import DstId, RemoteDMATransfer
 from concourse.mybir import AluOpType as OP, ActivationFunctionType as AF
 
 U, RO = 1024, 4
-PIECES = [(0, 256, 0), (256, 512, 1), (512, 1024, None)]
-SB = (0, 1)
-PS = (2, 3, 4, 5, 6, 7)
-ORDER = ("Y1' L0' B0 B1 e1' R1' G2 D0 G3 Z1' F0 O1' G4 F1 X0 L1' W2 K0 X1 W3 X2 G5 G6 X3 W4 K1 C0 W5 X4 G7 A0 G1 W6 X6 M0024 W7 X5 X7 "
-         "M0124 G0 M0224 D1 C1 A1 M0002 M0102 S00 M0324 S01 M0202 M0302 S02 M1004 M1104 S03 T0 M1204 N0 S10 S11 e0 M1304 S12 Y0 S13 "
-         "R0 T1 Z0 N1 O0").split()
+PIECES = [(0, 256, 0, (1, 2, 3)), (256, 512, 1, (1, 2, 3)), (512, 1024, None, (1, 2, 3))]
+FIRST = [(0, 192, 0, (1, 2, 3)), (192, 384, 1, (1, 2, 3)), (384, 1024, None, (1, 2, 3))]
+LATE = 0
+ALL16 = 1
+ORDER = ("Y1' H1' E1' I1' O0' J1' L0' Z1' F0 G2 B0 G3 O1' K0 F1 W2 W3 B1 F6 X0 D0 X1 X2 G5 X3 G4 X6 C0 W4 L1' A0 G7 G0 X4 W5 X5 W7 X7 "
+         "M0024 G1 M0324 M0124 M0224 G6 V0 C1 M0002 A1 M0102 M0202 M0302 M11 S00 S01 S02 S03 M10 T0 K1 M12 N0 D1 E0 V1 S11 Q0 M13 Y0 "
+         "S12 I0 S10 S13 H0 T1 Q1 J0 N1 Z0").split()
+ORDER0 = [x for x in ORDER if "'" not in x]
+ORDER3 = ORDER + "E1 Y1 H1 I1 O0 J1 Z1 O1".split()
+ORDERS = [ORDER0, ORDER, ORDER, ORDER3]
+FUSED = [[b for b in range(8) if "F%d" % b in order] for order in ORDERS]
 
 SCRATCH = {}
-for _n in ("W0", "W1", "W2"):
-    SCRATCH[_n] = ("psum", [128, 1024], "bfloat16")
-for _n in ("X0", "X1", "K0", "K1", "DD"):
+for _n in ("X0", "X1", "K0", "K1", "D0", "D1", "R0", "R1"):
     SCRATCH[_n] = ("psum", [128, 512], "float32")
 for _n, _w, _d in (
         ("win0", 4096, "bfloat16"), ("win1", 4096, "bfloat16"), ("win2", 4096, "bfloat16"), ("win3", 4096, "bfloat16"),
         ("vo", 1024, "bfloat16"), ("p", 4096, "bfloat16"), ("wp", 4096, "float16"), ("pv", 4096, "float32"),
-        ("wsb", 4096, "bfloat16"), ("wi", 1024, "int32"), ("wb", 1024, "bfloat16"), ("bi", 512, "int32"), ("bh", 512, "float16"),
-        ("lraw", 256, "int32"), ("off", 256, "uint16"), ("lf", 256, "float32"), ("ly", 256, "float32"), ("yb", 1024, "float32"),
-        ("z1", 128, "bfloat16"), ("z2", 128, "bfloat16"), ("z3", 128, "bfloat16"), ("z4", 16, "bfloat16"), ("ge", 16, "float32"),
-        ("fs", 512, "bfloat16"), ("fh", 256, "float16"), ("ih", 128, "float16"), ("ib", 128, "bfloat16"),
-        ("dm", 256, "float32"), ("bm", 160, "float32"), ("tmp", 128, "bfloat16"), ("tm2", 128, "bfloat16"),
-        ("bk", 32, "float32"), ("rst", 272, "float32"), ("ones", 128, "bfloat16"), ("koff", 272, "bfloat16"), ("c255", 4, "float32")):
+        ("wsb", 4096, "bfloat16"), ("yb", 1024, "bfloat16"), ("c255", 4, "float32"), ("ti", 512, "int32"), ("tb", 512, "float16"),
+        ("off", 256, "uint16"), ("lf", 256, "float16"),
+        ("z1", 128, "bfloat16"), ("zW", 128, "bfloat16"), ("zB", 128, "bfloat16"), ("z4", 16, "bfloat16"), ("ge", 16, "float32"),
+        ("fs", 1024, "float16"), ("fb", 256, "float16"), ("fw", 256, "float16"), ("f01", 256, "float16"), ("f23", 256, "float16"),
+        ("ih", 128, "float16"), ("ib", 128, "bfloat16"), ("ident", 128, "float32"),
+        ("tmp", 128, "bfloat16"), ("tm2", 128, "bfloat16"),
+        ("bk", 32, "float32"), ("svm", 8, "bfloat16"), ("rst", 272, "float32"), ("ones", 128, "bfloat16"), ("koff", 400, "bfloat16"),
+        ("bm", 128, "float16")):
     SCRATCH[_n] = ("sbuf", [128, _w], _d)
+SCRATCH["dm"] = ("sbuf", [128, 64, 5], "float16")
+SCRATCH["lraw"] = ("sbuf", [128, 4, 2, 32], "int32")
+SCRATCH["ly"] = ("sbuf", [128, 4, 2, 32], "float32")
 for _h in range(2):
-    for _n, _w, _d in (("mx", 272, "float32"), ("ne", 256, "float32"), ("yy", 256, "float32"), ("ew", 128, "float32"),
-                       ("sk", 128, "float32"), ("tt", 128, "float32"), ("aa", 64, "float32"), ("ai", 64, "int32")):
+    for _n, _w, _d in (("mx", 272, "float32"), ("ne", 320, "float32"), ("yy", 320, "float32"), ("ew", 160, "float32"),
+                       ("sk", 128, "float32"), ("tt", 128, "float32"), ("ai", 64, "int32")):
         SCRATCH["%s%d" % (_n, _h)] = ("sbuf", [128, _w], _d)
 
-SEMAPHORES = ["V", "S", "P", "G", "la0", "la1", "lw", "lb", "ls", "st", "sent", "arr0", "arr1", "arr2", "arr3"]
+SEMAPHORES = ["V", "S", "P", "G", "la0", "la1", "lt", "ls", "st", "sent", "hand0", "hand1", "arr0", "arr1", "arr2", "arr3"]
 
 
 def bits(engines):
@@ -46,23 +54,26 @@ def helpers_of(core, cores, topo):
     return sorted(able, key=lambda c: topo.die(c) == topo.die(core))
 
 
-def fan_out(g, T, topo, src, rank, ap, sem):
+def pieces(r):
+    return PIECES if r else FIRST
+
+
+def fan_out(g, T, topo, src, rank, ap, sem, to):
     n = len(T.cores)
-    dsts = [T.cores[(rank + k) % n] for k in range(1, n)]
+    dsts = [T.cores[(rank + k) % n] for k in to]
     eng = topo.engines(src, dsts[0])
     g.remote_dma_fused([RemoteDMATransfer(dst_ids=[dst_id(d, topo) for d in dsts], dma_engine_mask=bits(eng), remote_sem=sem,
                                           src=ap, dsts=[ap] * len(dsts))], local_sem=T.sem.sent)
     return len(eng)
 
 
-def hand_engines(core, cores, topo, r, h):
+def hand_engines(core, cores, topo, r):
     eng = topo.engines(core, helpers_of(core, cores, topo)[0])
-    vias = [via for c0, c1, via in PIECES if c0 // 512 == h]
-    if r == 0 or None in vias:
+    if r == 0 and not ALL16:
         far = topo.engines(core, [c for c in cores if c != core][0])
         eng = [e for e in eng if e not in far]
-    vias = [via for via in vias if via is not None]
-    n = len(eng) // len(vias)
+    vias = [via for c0, c1, via, to in pieces(r) if via is not None]
+    n = len(eng) // (len(vias) + len(vias) // 3)
     return {via: eng[i * n:i * n + n] for i, via in enumerate(vias)}
 
 
@@ -70,10 +81,10 @@ def helper_program(g, core, owner, k, T, topo):
     rank = T.rank_of(owner)
     sent = 0
     for r in range(RO):
-        for c0, c1, via in PIECES:
+        for c0, c1, via, to in pieces(r):
             if via == k:
-                g.wait_ge(T.sem["arr%d" % r], len(hand_engines(owner, T.cores, topo, r, c0 // 512)[k]))
-                sent += fan_out(g, T, topo, core, rank, T["win%d" % r][:, rank * U + c0:rank * U + c1], T.sem["arr%d" % r])
+                g.wait_ge(T.sem["arr%d" % r], len(hand_engines(owner, T.cores, topo, r)[k]))
+                sent += fan_out(g, T, topo, core, rank, T["win%d" % r][:, rank * U + c0:rank * U + c1], T.sem["arr%d" % r], to)
     if sent:
         g.wait_ge(T.sem.sent, sent)
 
@@ -89,11 +100,8 @@ def rank_program(g, core, T, topo):
     cores = T.cores
     R = rank * U
     helpers = helpers_of(core, cores, topo)
-    n_arr = 0
-    for c in cores:
-        if c != core:
-            for c0, c1, via in PIECES:
-                n_arr += len(topo.engines(c if via is None else helpers_of(c, cores, topo)[via], core))
+    n_arr = [sum(len(topo.engines(c if via is None else helpers_of(c, cores, topo)[via], core))
+                 for q, c in enumerate(cores) if c != core for c0, c1, via, to in pieces(r) if (rank - q) % len(cores) in to) for r in range(RO)]
 
     Q = {"V": g.vector, "S": g.scalar, "P": g.tensor, "G": g, "Y": g.sync}
     cnt = {"V": 0, "S": 0, "P": 0, "G": 0}
@@ -148,40 +156,46 @@ def rank_program(g, core, T, topo):
         note(q, (sem, total), rd, wr, ())
 
     V, S, P = g.vector, g.scalar, g.tensor
-    sent = [0]
+    sent, handed = [0], [0]
 
     def send(r, h):
         need("G", [lastw["v%d%d" % (r, h)]])
         sem = T.sem["arr%d" % r]
         hand = []
-        for c0, c1, via in PIECES:
-            if c0 // 512 == h and via is not None:
+        for c0, c1, via, to in pieces(r):
+            if (c1 - 1) // 512 == h and via is not None:
                 ap = T["win%d" % r][:, R + c0:R + c1]
-                eng = hand_engines(core, cores, topo, r, h)[via]
+                eng = hand_engines(core, cores, topo, r)[via]
                 hand.append(RemoteDMATransfer(dst_ids=[dst_id(helpers[via], topo)], dma_engine_mask=bits(eng), remote_sem=sem, src=ap, dst=ap))
-                sent[0] += len(eng)
+                handed[0] += len(eng)
         if hand:
-            g.remote_dma_fused(hand, local_sem=T.sem.sent)
-        for c0, c1, via in PIECES:
-            if c0 // 512 == h and via is None:
-                sent[0] += fan_out(g, T, topo, core, rank, T["win%d" % r][:, R + c0:R + c1], sem)
+            g.remote_dma_fused(hand, local_sem=T.sem["hand%d" % min(r, 1)])
+        for c0, c1, via, to in pieces(r):
+            if (c1 - 1) // 512 == h and via is None:
+                sent[0] += fan_out(g, T, topo, core, rank, T["win%d" % r][:, R + c0:R + c1], sem, to)
 
     dma("Y", T.win0[:, R:R + 512], T.a0[:, 0:512], "la0", 16, wr=["v00"])
     dma("S", T.win0[:, R + 512:R + U], T.a0[:, 512:U], "la1", 16, wr=["v01"])
-    dma("Y", T.wi[0:32, :], T.wt[:, :], "lw", 16, wr=["wi"])
-    dma("S", T.bi[0:16, :], T.bs[:, :], "lb", 16, wr=["bi"])
+    dma("Y", T.ti[0:64, :], T.wt[:, :], "lt", 32, wr=["tiw"])
+    dma("S", T.ti[64:80, :], T.bs[:, :], "lt", 32, wr=["tib"])
     for a in range(4):
-        dma("YS"[a % 2], T.lraw[:, 64 * a:64 * a + 64], T.sr[a::4, :], "ls", 64, wr=["lraw%d" % a])
+        if not LATE:
+            dma("YS"[a % 2], T.lraw[:, a, :, :], T.sr[a::4, :], "ls", 64, wr=["lraw%d" % a])
 
     imp = {"allow_small_or_imprecise_dtypes": True}
-    op("G", lambda: g.iota(T.z2[0:32, :], [[-4, 8], [0, 16]], 0, 1, **imp), wr=["z2"])
+    op("G", lambda: g.iota(T.zW[0:80, :], [[-8, 8], [0, 16]], 0, 1, **imp), wr=["zW"])
     op("G", lambda: g.iota(T.z1[:, :], [[1, 128]], 0, -1, **imp), wr=["z1"])
-    op("G", lambda: g.iota(T.z3[0:16, :], [[-2, 8], [0, 16]], 0, 1, **imp), wr=["z3"])
+    op("G", lambda: g.iota(T.zB[0:80, :], [[-2, 8], [0, 16]], 0, 1, **imp), wr=["zB"])
     op("G", lambda: g.iota(T.z4[:, 0:16], [[-16, 16]], 0, 1, **imp), wr=["z4"])
     send(0, 0)
     send(0, 1)
+    hand0 = handed[0]
     for r in range(RO):
-        lastw["arr%d" % r] = ("arr%d" % r, n_arr)
+        lastw["arr%d" % r] = ("arr%d" % r, n_arr[r])
+    if LATE:
+        need("Y", [("hand0", hand0)] if LATE == 1 else [lastw["v00"], lastw["v01"]])
+        for a in range(4):
+            dma("Y", T.lraw[:, a, :, :], T.sr[a::4, :], "ls", 64, wr=["lraw%d" % a])
 
     def ts(out, in0, s1, op0, rd, wr, s2=None, op1=None, banks=()):
         if op1 is None:
@@ -201,69 +215,68 @@ def rank_program(g, core, T, topo):
     def mm(out, lhsT, rhs, start, stop, rd, wr, banks):
         op("P", lambda: P.matmul(out, lhsT, rhs, start, stop), rd, wr, banks)
 
+    def fill(ap, value, key):
+        op("V", lambda: V.memset(ap, value), wr=[key])
+
     def four(name):
         return [name + str(i) for i in range(4)]
 
-    op("V", lambda: V.memset(T.rst[:, :], 0.0), wr=["rst"])
-    op("V", lambda: V.memset(T.ones[0:1, :], 1.0), wr=["ones"])
-    op("V", lambda: V.memset(T.c255[:, :], 255.0), wr=["c255"])
+    fill(T.rst[:, :], 0.0, "rst")
+    fill(T.ones[0:1, :], 1.0, "ones")
+    fill(T.c255[:, :], 255.0, "c255")
     for s in range(4):
-        op("V", lambda: V.memset(T.koff[0:1, s::4], (1.5 - s) / 4), wr=["koff%d" % s])
-    op("V", lambda: V.memset(T.rst[:, 0::4], -4194304.0), wr=["rst"])
+        fill(T.koff[0:1, s:272:4], (1.5 - s) / 4, "koff%d" % s)
+    fill(T.koff[0:1, 272:400], 2048.0, "koff4")
+    for h in range(2):
+        fill(T["ne%d" % h][:, 4::5], 1.0, "one%d" % h)
+    fill(T.rst[:, 0::4], -4194304.0, "rst")
     for s in range(4):
-        ts(T.fs[0:32, 128 * s:128 * s + 128], T.z2[0:32, :], float(s), OP.is_equal, ["z2"], ["fs%d" % s])
-    ident = T.bm[:, 32:160]
+        for h in range(2):
+            ts(T.fs[0:80, 256 * s + 128 * h:256 * s + 128 * h + 128], T.zW[0:80, :], float(2 * s + h), OP.is_equal, ["zW"], ["fs%d%d" % (s, h)])
+    for h in range(2):
+        ts(T.fb[0:80, 128 * h:128 * h + 128], T.zB[0:80, :], float(64 + h), OP.is_equal, ["zB"], ["fb%d" % h])
     ts(T.ib[:, :], T.z1[:, :], 0.0, OP.is_equal, ["z1"], ["ib"])
     ts(T.tmp[:, :], T.z1[:, :], 1.0, OP.is_equal, ["z1"], ["tmp"])
-    ts(T.ih[:, :], T.z1[:, :], 0.0, OP.is_equal, ["z1"], ["ih"])
-    tt(T.tm2[:, :], T.tmp[:, :], T.ib[:, :], OP.subtract, ["tmp", "ib"], ["tm2"])
-    for h in range(2):
-        ts(T.fh[0:16, 128 * h:128 * h + 128], T.z3[0:16, :], float(h), OP.is_equal, ["z3"], ["fh%d" % h])
+    ts(T.ih[:, :], T.z1[:, :], 0.0, OP.is_equal, ["z1"], ["ih"], 1024.0, OP.mult)
+    ts(T.bm[:, :], T.z1[:, :], 0.0, OP.is_equal, ["z1"], ["bm"])
+    ts(T.dm[:, 0:32, 4], T.z1[:, 3::4], 0.0, OP.mult, ["z1"], ["dm2"])
+    ts(T.dm[:, 32:64, 4], T.z1[:, 3::4], 0.0, OP.is_equal, ["z1"], ["dm3"], 20.0, OP.mult)
+    tt(T.f01[0:80, :], T.fs[0:80, 0:256], T.fs[0:80, 256:512], OP.add, ["fs00", "fs01", "fs10", "fs11"], ["f01"])
+    act(T.ident[:, :], T.ib[:, :], ["ib"], ["ident"])
+    tt(T.f23[0:80, :], T.fs[0:80, 512:768], T.fs[0:80, 768:1024], OP.add, ["fs20", "fs21", "fs30", "fs31"], ["f23"])
     ts(T.ge[:, :], T.z4[:, :], 0.0, OP.is_ge, ["z4"], ["ge"])
-    act(ident, T.ib[:, :], ["ib"], ["ident"])
-    act(T.bm[:, 0:32], T.ib[:, 3::4], ["ib"], ["base"], scale=20.0)
-    act(T.dm[:, 0:128], T.tm2[:, :], ["tm2"], ["dm0"], scale=7.0)
-    act(T.dm[:, 128:256], T.tm2[:, :], ["tm2"], ["dm1"], scale=13.0)
-    tt(T.bk[:, 0:8], T.ge[:, 1:9], T.ge[:, 0:8], OP.subtract, ["ge"], ["bk0"])
-    tt(T.bk[:, 8:16], T.ge[:, 0:8], T.ge[:, 1:9], OP.subtract, ["ge"], ["bk1"])
-    tt(T.bk[:, 16:17], T.ge[:, 0:1], T.ge[:, 1:2], OP.subtract, ["ge"], ["bk2"])
-    for h in range(2):
-        vcopy(T.wb[0:32, 512 * h:512 * h + 512], T.wi[0:32, 512 * h:512 * h + 512], ["wi"], ["wb%d" % h])
-
-    def wcols(b):
-        c = 512 * (SB + PS).index(b)
-        return slice(c, c + 512)
-
-    def weights(b, bank, copy):
-        h, a = divmod(b, 4)
-        for s in range(4):
-            mm(T[bank][:, s::4], T.fs[0:32, 128 * s:128 * s + 128], T.wb[0:32, 512 * h + a:512 * h + 512:4], True, True,
-               ["fs%d" % s, "wb%d" % h], ["stg%s%d" % (bank, s)], [bank])
-        return lambda: copy(T.wsb[:, wcols(b)], T[bank][:, :], four("stg" + bank), ["ws%d" % b], [bank])
-
-    def weights_to_psum(k):
-        vcopy(T["W%d" % k][:, :], T.wsb[:, 1024 * (k + 1):1024 * (k + 2)], ["ws%d" % b for b in PS[2 * k:2 * k + 2]], ["W%d" % k], ["W%d" % k])
-
-    weights(PS[0], "X0", act)()
-    weights(PS[1], "X1", act)()
-    later = weights(SB[0], "K0", vcopy)
-    for b, bank in ((SB[1], "K1"), (PS[2], "DD"), (PS[3], "X0"), (PS[4], "X1"), (PS[5], "K1")):
-        weights(b, bank, act)()
-    for a in range(4):
-        for h in range(2):
-            vcopy(T.off[:, 128 * h + 32 * a:128 * h + 32 * a + 32], T.lraw[:, 64 * a + 32 * h:64 * a + 32 * h + 32],
-                  ["lraw%d" % a], ["offi%d%d" % (h, a)])
-    later()
-    weights_to_psum(0)
-    for a in range(4):
-        vcopy(T.bh[0:16, 128 * a:128 * a + 128], T.bi[0:16, a::4], ["bi"], ["bh%d" % a])
-    for h in range(2):
-        vcopy(T.lf[:, 128 * h:128 * h + 128], T.off[:, 128 * h:128 * h + 128], four("offi%d" % h), ["lf%d" % h, "off%d" % h])
-    weights_to_psum(1)
-    weights_to_psum(2)
+    vcopy(T.tb[0:80, :], T.ti[0:80, :], ["tiw", "tib"], ["tb"])
+    tt(T.f01[0:80, :], T.f01[0:80, :], T.f23[0:80, :], OP.add, ["f23"], ["f01"])
+    tt(T.tm2[:, :], T.tmp[:, :], T.ib[:, :], OP.subtract, ["tmp", "ib"], ["tm2"])
 
     def cols(b):
         return slice(512 * b, 512 * b + 512)
+
+    for b, bank in enumerate(("R0", "R1", "D0", "X0", "X1", "K0", "K1", "D1")):
+        h, a = divmod(b, 4)
+        for s in range(4):
+            mm(T[bank][:, s::4], T.fs[0:80, 256 * s + 128 * h:256 * s + 128 * h + 128], T.tb[0:80, a::4], True, True,
+               ["fs%d%d" % (s, h), "tb"], ["stg%s%d" % (bank, s)], [bank])
+        if b % 3 == 1:
+            ts(T.wsb[:, cols(b)], T[bank][:, :], 1.0 / 1024, OP.mult, four("stg" + bank), ["ws%d" % b], banks=[bank])
+        else:
+            act(T.wsb[:, cols(b)], T[bank][:, :], four("stg" + bank), ["ws%d" % b], [bank], scale=1.0 / 1024)
+
+    def list_half(h):
+        ts(T.lf[:, 128 * h:128 * h + 128], T.off[:, 128 * h:128 * h + 128], -2048.0, OP.add, ["off%d" % h], ["lf%d" % h])
+
+    ts(T.fw[0:80, :], T.f01[0:80, :], -1.0, OP.mult, ["f01"], ["fw"])
+    ts(T.dm[:, 0:32, 0:4], T.tm2[:, :], 7.0, OP.mult, ["tm2"], ["dm0"])
+    ts(T.dm[:, 32:64, 0:4], T.tm2[:, :], 13.0, OP.mult, ["tm2"], ["dm1"])
+    tt(T.bk[:, 0:8], T.ge[:, 1:9], T.ge[:, 0:8], OP.subtract, ["ge"], ["bk0"])
+    tt(T.bk[:, 8:16], T.ge[:, 0:8], T.ge[:, 1:9], OP.subtract, ["ge"], ["bk1"])
+    tt(T.bk[:, 16:17], T.ge[:, 0:1], T.ge[:, 1:2], OP.subtract, ["ge"], ["bk2"])
+    vcopy(T.svm[:, 0:7], T.bk[:, 1:8], ["bk0"], ["svm0"])
+    vcopy(T.svm[:, 7:8], T.bk[:, 0:1], ["bk0"], ["svm1"])
+    for h in range(2):
+        vcopy(T.off[:, 128 * h:128 * h + 128], T.lraw[:, :, h, :], four("lraw"), ["off%d" % h])
+    list_half(0)
+    list_half(1)
 
     def gathered(r, b):
         return T["win%d" % r][:, 0:4096].indirect(T.off[:, 32 * b:32 * b + 32])
@@ -272,22 +285,24 @@ def rank_program(g, core, T, topo):
         return ["arr%d" % r, "v%d0" % r, "v%d1" % r, "off%d" % (b // 4)]
 
     def gather(r, b):
-        op("S", lambda: S.activation(T.p[:, cols(b)], gathered(r, b), AF.Copy), win_keys(r, b), ["p%d" % b])
+        if b in FUSED[r]:
+            act(T.p[:, cols(b)], gathered(r, b), win_keys(r, b), ["p%d" % b])
+        else:
+            act(T.p[:, cols(b)], gathered(r, b), win_keys(r, b), ["p%d" % b], (), AF.Identity, 1.0, 1.0)
 
     def gather_weigh(r, b):
-        tt(T.wp[:, cols(b)], gathered(r, b), T.wsb[:, wcols(b)], OP.mult, win_keys(r, b) + ["ws%d" % b], ["wp%d" % b])
+        tt(T.wp[:, cols(b)], gathered(r, b), T.wsb[:, cols(b)], OP.mult, win_keys(r, b) + ["ws%d" % b], ["wp%d" % b])
 
     def weigh(r, b):
-        if b in SB:
-            tt(T.wp[:, cols(b)], T.p[:, cols(b)], T.wsb[:, wcols(b)], OP.mult, ["p%d" % b, "ws%d" % b], ["wp%d" % b])
-        else:
-            k, half = divmod(PS.index(b), 2)
-            tt(T.wp[:, cols(b)], T.p[:, cols(b)], T["W%d" % k][:, 512 * half:512 * half + 512], OP.mult,
-               ["p%d" % b, "W%d" % k], ["wp%d" % b], ["W%d" % k])
+        op("V", lambda: V.tensor_tensor_scan(T.wp[:, cols(b)], T.p[:, cols(b)], T.wsb[:, cols(b)], 0.0, OP.max, OP.mult),
+           ["p%d" % b, "ws%d" % b], ["wp%d" % b])
 
     def bias(r, h):
-        mm(T["X%d" % h][:, :], T.fh[0:16, 128 * h:128 * h + 128], T.bh[0:16, :], True, False,
-           ["fh%d" % h] + four("bh"), ["xb%d" % h, "xv%d" % h], ["X%d" % h])
+        X = T["X%d" % h]
+        mm(X[:, :], T.fb[0:80, 128 * h:128 * h + 128], T.tb[0:80, :], True, False, ["fb%d" % h, "tb"], ["xb%d" % h, "xv%d" % h], ["X%d" % h])
+        for a in range(4):
+            if 4 * h + a not in FUSED[r]:
+                mm(X[:, a::4], T.fw[0:80, 128 * h:128 * h + 128], T.tb[0:80, a::4], False, False, ["fw"], ["xb%d" % h], ["X%d" % h])
 
     done = {}
 
@@ -299,43 +314,39 @@ def rank_program(g, core, T, topo):
         h, a = divmod(b, 4)
         last = closes(("x", r, h))
         for s in range(4):
-            mm(T["X%d" % h][:, 128 * a:128 * a + 128], T.ih[:, :], T.wp[:, 512 * b + s:512 * b + 512:4], False, last and s == 3,
+            mm(T["X%d" % h][:, a::4], T.ih[:, :], T.wp[:, 512 * b + s:512 * b + 512:4], False, last and s == 3,
                ["ih", "wp%d" % b, "xb%d" % h], ["x%d%d" % (h, a)], ["X%d" % h])
 
     def diffs(r, h):
-        mm(T.DD[:, 256 * h:256 * h + 256], T.lf[:, 128 * h:128 * h + 128], T.dm[:, :], True, True,
-           ["lf%d" % h, "dm0", "dm1"], ["d%d" % h], ["DD"])
+        mm(T["D%d" % h][:, 0:320], T.lf[:, 128 * h:128 * h + 128], T.dm[:, :, :], True, False, ["lf%d" % h] + four("dm"), ["d%d" % h], ["D%d" % h])
 
     def keys_open(r, h):
         K = T["K%d" % h]
-        mm(K[:, 272:432], T.lf[:, 128 * h:128 * h + 128], T.bm[:, :], True, True, ["lf%d" % h, "ident", "base"], ["ks%d" % h], ["K%d" % h])
-        mm(K[:, 0:272], T.ones[0:1, :], T.koff[0:1, :], True, False, ["ones"] + four("koff"), ["kb%d" % h] + four("k%d" % h), ["K%d" % h])
+        mm(K[:, 0:400], T.ones[0:1, :], T.koff[0:1, :], True, False, ["ones", "koff4"] + four("koff"),
+           ["kb%d" % h, "ks%d" % h] + four("k%d" % h), ["K%d" % h])
+        mm(K[:, 272:400], T.lf[:, 128 * h:128 * h + 128], T.bm[:, :], False, False, ["lf%d" % h, "bm"], ["ks%d" % h], ["K%d" % h])
 
     def new_act(r, h):
         return (T.vo, 512 * h) if r == RO - 1 else (T["win%d" % (r + 1)], R + 512 * h)
 
-    def pass_on(r, h):
-        if r == RO - 1:
-            dma("Y", T.ya[:, 512 * h:512 * h + 512], T.vo[:, 512 * h:512 * h + 512], "st", 96, rd=["v%d%d" % (r + 1, h)])
-        else:
-            send(r + 1, h)
-
     def clamp(r, h):
         buf, c0 = new_act(r, h)
         key = "v%d%d" % (r + 1, h)
-        for a in range(4):
-            ts(buf[:, c0 + a:c0 + 512:4], T["X%d" % h][:, 128 * a:128 * a + 128], 0.0, OP.max, four("x%d" % h),
-               [key] if a == 3 else [key + "_%d" % a], 255.0, OP.min, ["X%d" % h])
-        pass_on(r, h)
+        ts(buf[:, c0:c0 + 512], T["X%d" % h][:, :], 0.0, OP.max, four("x%d" % h), [key], 255.0, OP.min, ["X%d" % h])
+        pass_on(r, h, key)
 
     def clamp_scalar(r, h):
         buf, c0 = new_act(r, h)
         key = "v%d%d" % (r + 1, h)
-        act(T.yb[:, 512 * h:512 * h + 512], T["X%d" % h][:, :], four("x%d" % h) + ["c255"], ["yb%d" % h], ["X%d" % h], AF.Relu, T.c255[:, 0:1], -1.0)
-        for a in range(4):
-            act(buf[:, c0 + a:c0 + 512:4], T.yb[:, 512 * h + 128 * a:512 * h + 128 * a + 128], ["yb%d" % h],
-                [key] if a == 3 else [key + "_%d" % a], (), AF.Relu, T.c255[:, 0:1], -1.0)
-        pass_on(r, h)
+        act(T.yb[:, cols(h)], T["X%d" % h][:, :], four("x%d" % h) + ["c255"], ["yb%d" % h], ["X%d" % h], AF.Relu, T.c255[:, 0:1], -1.0)
+        act(buf[:, c0:c0 + 512], T.yb[:, cols(h)], ["yb%d" % h], [key], (), AF.Relu, T.c255[:, 0:1], -1.0)
+        pass_on(r, h, key)
+
+    def pass_on(r, h, key):
+        if r == RO - 1:
+            dma("Y", T.ya[:, 512 * h:512 * h + 512], T.vo[:, 512 * h:512 * h + 512], "st", 96, rd=[key])
+        else:
+            send(r + 1, h)
 
     def act_to_psum(r, h):
         buf, c0 = new_act(r, h)
@@ -343,7 +354,15 @@ def rank_program(g, core, T, topo):
             mm(T["X%d" % h][:, 128 * a:128 * a + 128], T.ib[:, :], buf[:, c0 + a:c0 + 512:4], True, True,
                ["ib", "v%d%d" % (r + 1, h)], ["xv%d" % h], ["X%d" % h])
 
-    def prod(r, h, s, a0, a1):
+    def act_sums(r, h):
+        buf, c0 = new_act(r, h)
+        for a in range(4):
+            for cc in range(4):
+                if 4 * h + a not in FUSED[r]:
+                    mm(T["D%d" % h][32 * a:32 * a + 32, 164 + 5 * cc:320:20], buf[:, c0 + 4 * cc + a:c0 + 512:16], T.svm[:, :], False, False,
+                       ["svm0", "svm1", "v%d%d" % (r + 1, h)], ["d%d" % h], ["D%d" % h])
+
+    def prod(r, h, s, a0=0, a1=4):
         c = 2048 * h + 512 * s
         tt(T.pv[:, c + 128 * a0:c + 128 * a1], T.p[:, 2048 * h + 512 * a0 + s:2048 * h + 512 * a1:4], T["X%d" % h][:, 128 * a0:128 * a1],
            OP.mult, ["p%d" % (4 * h + a) for a in range(a0, a1)] + ["xv%d" % h], ["pv%d%d%d" % (h, s, a) for a in range(a0, a1)], ["X%d" % h])
@@ -360,60 +379,58 @@ def rank_program(g, core, T, topo):
            ["rst"] + four("k%d" % h), ["mx%d" % h], ["K%d" % h])
 
     def flags(r, h):
+        K, mx = T["K%d" % h], T["mx%d" % h]
         for s in range(4):
-            tt(T["ne%d" % h][:, s::4], T["K%d" % h][:, s:256:4], T["mx%d" % h][:, 3:256:4], OP.not_equal,
-               ["k%d%d" % (h, s), "mx%d" % h], ["ne%d%d" % (h, s)], ["K%d" % h])
+            tt(T["ne%d" % h][:, s::5], K[:, s:256:4], mx[:, 3:256:4], OP.not_equal, ["k%d%d" % (h, s), "mx%d" % h, "one%d" % h],
+               ["ne%d%d" % (h, s)], ["K%d" % h])
 
     def worst_scalar(r, h):
-        act(T["ew%d" % h][:, :], T["ne%d" % h][:, 0:128], four("ne%d" % h), ["ew%d" % h], (), AF.Identity, 1.0, -1.0)
+        act(T["ew%d" % h][:, :], T["ne%d" % h][:, 0:160], four("ne%d" % h), ["ew%d" % h], (), AF.Identity, 1.0, -1.0)
 
     def worst(r, h):
-        ts(T["ew%d" % h][:, :], T["ne%d" % h][:, 0:128], -1.0, OP.mult, four("ne%d" % h), ["ew%d" % h], 1.0, OP.add)
+        ts(T["ew%d" % h][:, :], T["ne%d" % h][:, 0:160], -1.0, OP.mult, four("ne%d" % h), ["ew%d" % h], 1.0, OP.add)
 
     def scan2(r, h):
-        op("V", lambda: V.tensor_tensor_scan(T["yy%d" % h][:, :], T.DD[:, 256 * h:256 * h + 256], T["ne%d" % h][:, :], 0.0, OP.add, OP.mult),
-           ["d%d" % h] + four("ne%d" % h), ["yy%d" % h], ["DD"])
+        op("V", lambda: V.tensor_tensor_scan(T["yy%d" % h][:, :], T["D%d" % h][:, 0:320], T["ne%d" % h][:, :], 0.0, OP.add, OP.mult),
+           ["d%d" % h] + four("ne%d" % h), ["yy%d" % h], ["D%d" % h])
 
-    def new_source(r, h):
-        K, aa, ai, yy = T["K%d" % h], T["aa%d" % h], T["ai%d" % h], T["yy%d" % h]
-        tt(aa[:, 32:64], T["mx%d" % h][:, 147:272:4], K[:, 272:304], OP.add, ["mx%d" % h, "ks%d" % h], ["a2%d" % h], ["K%d" % h])
-        tt(aa[:, 0:32], yy[:, 3:128:4], yy[:, 131:256:4], OP.add, ["yy%d" % h], ["a1%d" % h])
-        tt(T["sk%d" % h][:, :], T["ne%d" % h][:, 0:128], K[:, 304:432], OP.mult, four("ne%d" % h) + ["ks%d" % h], ["sk%d" % h], ["K%d" % h])
-        tt(ai[:, 0:32], aa[:, 0:32], aa[:, 32:64], OP.add, ["a1%d" % h, "a2%d" % h], ["a3%d" % h])
-        mm(K[:, 304:432], T["sk%d" % h][:, :], ident, True, False, ["sk%d" % h, "ident"], ["ks%d" % h], ["K%d" % h])
+    def base(r, h):
+        mm(T["D%d" % h][:, 164:320:5], T.ident[:, :], T["mx%d" % h][:, 147:272:4], False, True, ["mx%d" % h, "ident"], ["d%d" % h], ["D%d" % h])
+
+    def kept(r, h):
+        K = T["K%d" % h]
+        for s in range(4):
+            tt(T["sk%d" % h][:, s::4], T["ne%d" % h][:, s:160:5], K[:, 272 + s:400:4], OP.mult, ["ne%d%d" % (h, s), "ks%d" % h],
+               ["sk%d%d" % (h, s)], ["K%d" % h])
+        mm(K[:, 272:400], T["sk%d" % h][:, :], T.ident[:, :], True, False, four("sk%d" % h) + ["ident"], ["ks%d" % h], ["K%d" % h])
+
+    def to_int(r, h):
+        yy = T["yy%d" % h]
+        tt(T["ai%d" % h][:, 0:32], yy[:, 4:160:5], yy[:, 164:320:5], OP.add, ["yy%d" % h], ["a3%d" % h])
+
+    def modulo(r, h):
+        ai = T["ai%d" % h]
+        ts(ai[:, 32:64], ai[:, 0:32], 4095, OP.bitwise_and, ["a3%d" % h], ["a4%d" % h])
 
     def rewire(r, h):
-        K, ai = T["K%d" % h], T["ai%d" % h]
-        ts(ai[:, 32:64], ai[:, 0:32], 4095, OP.bitwise_and, ["a3%d" % h], ["a4%d" % h])
         for s in range(4):
-            tt(T["tt%d" % h][:, s::4], T["ew%d" % h][:, s::4], ai[:, 32:64], OP.mult, ["ew%d" % h, "a4%d" % h], ["tt%d%d" % (h, s)])
-        mm(K[:, 304:432], T["tt%d" % h][:, :], ident, False, True, four("tt%d" % h) + ["ident"], ["ks%d" % h], ["K%d" % h])
-
-    def sources_out(h, copy):
-        for a in range(4):
-            copy(T.ly[:, 64 * a + 32 * h:64 * a + 32 * h + 32], T["K%d" % h][:, 304 + 32 * a:336 + 32 * a], ["ks%d" % h],
-                 ["ly%d%d" % (h, a)], ["K%d" % h])
+            tt(T["tt%d" % h][:, s::4], T["ew%d" % h][:, s::5], T["ai%d" % h][:, 32:64], OP.mult, ["ew%d" % h, "a4%d" % h], ["tt%d%d" % (h, s)])
+        mm(T["K%d" % h][:, 272:400], T["tt%d" % h][:, :], T.ident[:, :], False, True, four("tt%d" % h), ["ks%d" % h], ["K%d" % h])
 
     def offsets(r, h):
-        if r < RO - 1:
-            vcopy(T.off[:, 128 * h:128 * h + 128], T["K%d" % h][:, 304:432], ["ks%d" % h], ["off%d" % h], ["K%d" % h])
-        elif h == 1:
-            sources_out(h, vcopy)
+        out, key = (T.off[:, 128 * h:128 * h + 128], "off%d" % h) if r < RO - 1 else (T.ly[:, :, h, :], "ly%d" % h)
+        vcopy(out, T["K%d" % h][:, 272:400], ["ks%d" % h], [key], ["K%d" % h])
 
-    def sources(r, h):
+    def list_step(r, h):
         if r < RO - 1:
-            act(T.lf[:, 128 * h:128 * h + 128], T["K%d" % h][:, 304:432], ["ks%d" % h], ["lf%d" % h], ["K%d" % h])
-        elif h == 0:
-            sources_out(h, act)
+            list_half(h)
 
     STEP = {"B": bias, "D": diffs, "K": keys_open, "F": gather_weigh, "G": gather, "W": weigh, "X": wsum, "C": clamp, "c": clamp_scalar,
-            "A": act_to_psum, "M": prod, "S": score, "T": scan1, "N": flags, "e": worst_scalar, "E": worst, "Y": scan2,
-            "R": new_source, "Z": rewire, "O": offsets, "L": sources}
-    for r in range(RO + 1):
-        for step in ORDER:
-            rr = r - step.count("'")
-            if 0 <= rr < RO:
-                STEP[step[0]](rr, *[int(c) for c in step[1:].strip("'")])
+            "A": act_to_psum, "V": act_sums, "M": prod, "S": score, "T": scan1, "N": flags, "E": worst_scalar, "e": worst, "Q": base, "H": kept,
+            "Y": scan2, "I": to_int, "J": modulo, "Z": rewire, "O": offsets, "L": list_step}
+    for r in range(RO):
+        for step in ORDERS[r]:
+            STEP[step[0]](r - step.count("'"), *[int(c) for c in step[1:].strip("'")])
     for a in range(4):
-        dma("YS"[a % 2], T.ys[a::4, :], T.ly[:, 64 * a:64 * a + 64], "st", 96, rd=["ly0%d" % a, "ly1%d" % a])
-    need("G", [("V", cnt["V"]), ("S", cnt["S"]), ("P", cnt["P"]), ("G", cnt["G"]), ("sent", sent[0]), ("st", 96)])
+        dma("YS"[a % 2], T.ys[a::4, :], T.ly[:, a, :, :], "st", 96, rd=["ly0", "ly1"])
+    need("G", [("V", cnt["V"]), ("S", cnt["S"]), ("P", cnt["P"]), ("G", cnt["G"]), ("sent", sent[0]), ("hand0", hand0), ("hand1", handed[0] - hand0), ("st", 96)])

from concourse.bass import DstId, RemoteDMATransfer
from concourse.mybir import AluOpType as OP, ActivationFunctionType as AF

U, RO = 1024, 4
PIECES = [(0, 256, 0, (1, 2, 3)), (256, 512, 1, (1, 2, 3)), (512, 1024, None, (1, 2, 3))]
FIRST = [(0, 192, 0, (1, 2, 3)), (192, 384, 1, (1, 2, 3)), (384, 1024, None, (1, 2, 3))]
LATE = 0
ALL16 = 1
ORDER = ("Y1' H1' E1' I1' O0' J1' L0' Z1' F0 G2 B0 G3 O1' K0 F1 W2 W3 B1 F6 X0 D0 X1 X2 G5 X3 G4 X6 C0 W4 L1' A0 G7 G0 X4 W5 X5 W7 X7 "
         "M0024 G1 M0324 M0124 M0224 G6 V0 C1 M0002 A1 M0102 M0202 M0302 M11 S00 S01 S02 S03 M10 T0 K1 M12 N0 D1 E0 V1 S11 Q0 M13 Y0 "
         "S12 I0 S10 S13 H0 T1 Q1 J0 N1 Z0").split()
ORDER0 = [x for x in ORDER if "'" not in x]
ORDER3 = ORDER + "E1 Y1 H1 I1 O0 J1 Z1 O1".split()
ORDERS = [ORDER0, ORDER, ORDER, ORDER3]
FUSED = [[b for b in range(8) if "F%d" % b in order] for order in ORDERS]

SCRATCH = {}
for _n in ("X0", "X1", "K0", "K1", "D0", "D1", "R0", "R1"):
    SCRATCH[_n] = ("psum", [128, 512], "float32")
for _n, _w, _d in (
        ("win0", 4096, "bfloat16"), ("win1", 4096, "bfloat16"), ("win2", 4096, "bfloat16"), ("win3", 4096, "bfloat16"),
        ("vo", 1024, "bfloat16"), ("p", 4096, "bfloat16"), ("wp", 4096, "float16"), ("pv", 4096, "float32"),
        ("wsb", 4096, "bfloat16"), ("yb", 1024, "bfloat16"), ("c255", 4, "float32"), ("ti", 512, "int32"), ("tb", 512, "float16"),
        ("off", 256, "uint16"), ("lf", 256, "float16"),
        ("z1", 128, "bfloat16"), ("zW", 128, "bfloat16"), ("zB", 128, "bfloat16"), ("z4", 16, "bfloat16"), ("ge", 16, "float32"),
        ("fs", 1024, "float16"), ("fb", 256, "float16"), ("fw", 256, "float16"), ("f01", 256, "float16"), ("f23", 256, "float16"),
        ("ih", 128, "float16"), ("ib", 128, "bfloat16"), ("ident", 128, "float32"),
        ("tmp", 128, "bfloat16"), ("tm2", 128, "bfloat16"),
        ("bk", 32, "float32"), ("svm", 8, "bfloat16"), ("rst", 272, "float32"), ("ones", 128, "bfloat16"), ("koff", 400, "bfloat16"),
        ("bm", 128, "float16")):
    SCRATCH[_n] = ("sbuf", [128, _w], _d)
SCRATCH["dm"] = ("sbuf", [128, 64, 5], "float16")
SCRATCH["lraw"] = ("sbuf", [128, 4, 2, 32], "int32")
SCRATCH["ly"] = ("sbuf", [128, 4, 2, 32], "float32")
for _h in range(2):
    for _n, _w, _d in (("mx", 272, "float32"), ("ne", 320, "float32"), ("yy", 320, "float32"), ("ew", 160, "float32"),
                       ("sk", 128, "float32"), ("tt", 128, "float32"), ("ai", 64, "int32")):
        SCRATCH["%s%d" % (_n, _h)] = ("sbuf", [128, _w], _d)

SEMAPHORES = ["V", "S", "P", "G", "la0", "la1", "lt", "ls", "st", "sent", "hand0", "hand1", "arr0", "arr1", "arr2", "arr3"]


def bits(engines):
    return sum(1 << e for e in engines)


def dst_id(c, topo):
    return DstId(rid=topo.addr(c)[0], pnc=topo.addr(c)[1])


def helpers_of(core, cores, topo):
    peers = [c for c in cores if c != core]
    able = [c for c in topo.cores_of(core) if c != core and all(topo.may_write(c, d) for d in peers)]
    return sorted(able, key=lambda c: topo.die(c) == topo.die(core))


def pieces(r):
    return PIECES if r else FIRST


def fan_out(g, T, topo, src, rank, ap, sem, to):
    n = len(T.cores)
    dsts = [T.cores[(rank + k) % n] for k in to]
    eng = topo.engines(src, dsts[0])
    g.remote_dma_fused([RemoteDMATransfer(dst_ids=[dst_id(d, topo) for d in dsts], dma_engine_mask=bits(eng), remote_sem=sem,
                                          src=ap, dsts=[ap] * len(dsts))], local_sem=T.sem.sent)
    return len(eng)


def hand_engines(core, cores, topo, r):
    eng = topo.engines(core, helpers_of(core, cores, topo)[0])
    if r == 0 and not ALL16:
        far = topo.engines(core, [c for c in cores if c != core][0])
        eng = [e for e in eng if e not in far]
    vias = [via for c0, c1, via, to in pieces(r) if via is not None]
    n = len(eng) // (len(vias) + len(vias) // 3)
    return {via: eng[i * n:i * n + n] for i, via in enumerate(vias)}


def helper_program(g, core, owner, k, T, topo):
    rank = T.rank_of(owner)
    sent = 0
    for r in range(RO):
        for c0, c1, via, to in pieces(r):
            if via == k:
                g.wait_ge(T.sem["arr%d" % r], len(hand_engines(owner, T.cores, topo, r)[k]))
                sent += fan_out(g, T, topo, core, rank, T["win%d" % r][:, rank * U + c0:rank * U + c1], T.sem["arr%d" % r], to)
    if sent:
        g.wait_ge(T.sem.sent, sent)


def rank_program(g, core, T, topo):
    rank = T.rank_of(core)
    if rank is None:
        for c in T.cores:
            hs = helpers_of(c, T.cores, topo)
            if core in hs:
                helper_program(g, core, c, hs.index(core), T, topo)
        return
    cores = T.cores
    R = rank * U
    helpers = helpers_of(core, cores, topo)
    n_arr = [sum(len(topo.engines(c if via is None else helpers_of(c, cores, topo)[via], core))
                 for q, c in enumerate(cores) if c != core for c0, c1, via, to in pieces(r) if (rank - q) % len(cores) in to) for r in range(RO)]

    Q = {"V": g.vector, "S": g.scalar, "P": g.tensor, "G": g, "Y": g.sync}
    cnt = {"V": 0, "S": 0, "P": 0, "G": 0}
    clock = {q: {} for q in Q}
    snap = {}
    lastw, readers, bankuse = {}, {}, {}

    def need(q, toks):
        best = {}
        for s, n in toks:
            if clock[q].get(s, 0) < n and best.get(s, 0) < n:
                best[s] = n
        for s, n in sorted(best.items(), key=lambda x: -len(snap.get(x, {}))):
            if clock[q].get(s, 0) >= n:
                continue
            Q[q].wait_ge(T.sem[s], n)
            clock[q][s] = n
            for s2, n2 in snap.get((s, n), {}).items():
                if clock[q].get(s2, 0) < n2:
                    clock[q][s2] = n2

    def deps(q, rd, wr, banks):
        toks = [lastw[k] for k in list(rd) + list(wr) if k in lastw]
        for k in wr:
            toks.extend(readers.get(k, []))
        if q == "P":
            toks = [t for t in toks if t[0] != "P"]
        for b in banks:
            toks.extend(t for e, t in bankuse.get(b, {}).items() if e != q)
        return toks

    def note(q, tok, rd, wr, banks):
        for k in rd:
            readers.setdefault(k, []).append(tok)
        for k in wr:
            lastw[k] = tok
            readers[k] = []
        for b in banks:
            bankuse.setdefault(b, {})[q] = tok

    def op(q, fn, rd=(), wr=(), banks=()):
        need(q, deps(q, rd, wr, banks))
        cnt[q] += 1
        tok = (q, cnt[q])
        fn().then_inc(T.sem[q], 1)
        snap[tok] = dict(clock[q])
        note(q, tok, rd, wr, banks)

    def dma(q, out, in_, sem, total, rd=(), wr=()):
        need(q, deps(q, rd, wr, ()))
        Q[q].dma_start(out, in_).then_inc(T.sem[sem], 16)
        note(q, (sem, total), rd, wr, ())

    V, S, P = g.vector, g.scalar, g.tensor
    sent, handed = [0], [0]

    def send(r, h):
        need("G", [lastw["v%d%d" % (r, h)]])
        sem = T.sem["arr%d" % r]
        hand = []
        for c0, c1, via, to in pieces(r):
            if (c1 - 1) // 512 == h and via is not None:
                ap = T["win%d" % r][:, R + c0:R + c1]
                eng = hand_engines(core, cores, topo, r)[via]
                hand.append(RemoteDMATransfer(dst_ids=[dst_id(helpers[via], topo)], dma_engine_mask=bits(eng), remote_sem=sem, src=ap, dst=ap))
                handed[0] += len(eng)
        if hand:
            g.remote_dma_fused(hand, local_sem=T.sem["hand%d" % min(r, 1)])
        for c0, c1, via, to in pieces(r):
            if (c1 - 1) // 512 == h and via is None:
                sent[0] += fan_out(g, T, topo, core, rank, T["win%d" % r][:, R + c0:R + c1], sem, to)

    dma("Y", T.win0[:, R:R + 512], T.a0[:, 0:512], "la0", 16, wr=["v00"])
    dma("S", T.win0[:, R + 512:R + U], T.a0[:, 512:U], "la1", 16, wr=["v01"])
    dma("Y", T.ti[0:64, :], T.wt[:, :], "lt", 32, wr=["tiw"])
    dma("S", T.ti[64:80, :], T.bs[:, :], "lt", 32, wr=["tib"])
    for a in range(4):
        if not LATE:
            dma("YS"[a % 2], T.lraw[:, a, :, :], T.sr[a::4, :], "ls", 64, wr=["lraw%d" % a])

    imp = {"allow_small_or_imprecise_dtypes": True}
    op("G", lambda: g.iota(T.zW[0:80, :], [[-8, 8], [0, 16]], 0, 1, **imp), wr=["zW"])
    op("G", lambda: g.iota(T.z1[:, :], [[1, 128]], 0, -1, **imp), wr=["z1"])
    op("G", lambda: g.iota(T.zB[0:80, :], [[-2, 8], [0, 16]], 0, 1, **imp), wr=["zB"])
    op("G", lambda: g.iota(T.z4[:, 0:16], [[-16, 16]], 0, 1, **imp), wr=["z4"])
    send(0, 0)
    send(0, 1)
    hand0 = handed[0]
    for r in range(RO):
        lastw["arr%d" % r] = ("arr%d" % r, n_arr[r])
    if LATE:
        need("Y", [("hand0", hand0)] if LATE == 1 else [lastw["v00"], lastw["v01"]])
        for a in range(4):
            dma("Y", T.lraw[:, a, :, :], T.sr[a::4, :], "ls", 64, wr=["lraw%d" % a])

    def ts(out, in0, s1, op0, rd, wr, s2=None, op1=None, banks=()):
        if op1 is None:
            op("V", lambda: V.tensor_scalar(out, in0, s1, None, op0), rd, wr, banks)
        else:
            op("V", lambda: V.tensor_scalar(out, in0, s1, s2, op0, op1), rd, wr, banks)

    def tt(out, in0, in1, o, rd, wr, banks=()):
        op("V", lambda: V.tensor_tensor(out, in0, in1, o), rd, wr, banks)

    def vcopy(out, in_, rd, wr, banks=()):
        op("V", lambda: V.tensor_copy(out, in_), rd, wr, banks)

    def act(out, in_, rd, wr, banks=(), f=AF.Copy, bias=0.0, scale=1.0):
        op("S", lambda: S.activation(out, in_, f, bias, scale), rd, wr, banks)

    def mm(out, lhsT, rhs, start, stop, rd, wr, banks):
        op("P", lambda: P.matmul(out, lhsT, rhs, start, stop), rd, wr, banks)

    def fill(ap, value, key):
        op("V", lambda: V.memset(ap, value), wr=[key])

    def four(name):
        return [name + str(i) for i in range(4)]

    fill(T.rst[:, :], 0.0, "rst")
    fill(T.ones[0:1, :], 1.0, "ones")
    fill(T.c255[:, :], 255.0, "c255")
    for s in range(4):
        fill(T.koff[0:1, s:272:4], (1.5 - s) / 4, "koff%d" % s)
    fill(T.koff[0:1, 272:400], 2048.0, "koff4")
    for h in range(2):
        fill(T["ne%d" % h][:, 4::5], 1.0, "one%d" % h)
    fill(T.rst[:, 0::4], -4194304.0, "rst")
    for s in range(4):
        for h in range(2):
            ts(T.fs[0:80, 256 * s + 128 * h:256 * s + 128 * h + 128], T.zW[0:80, :], float(2 * s + h), OP.is_equal, ["zW"], ["fs%d%d" % (s, h)])
    for h in range(2):
        ts(T.fb[0:80, 128 * h:128 * h + 128], T.zB[0:80, :], float(64 + h), OP.is_equal, ["zB"], ["fb%d" % h])
    ts(T.ib[:, :], T.z1[:, :], 0.0, OP.is_equal, ["z1"], ["ib"])
    ts(T.tmp[:, :], T.z1[:, :], 1.0, OP.is_equal, ["z1"], ["tmp"])
    ts(T.ih[:, :], T.z1[:, :], 0.0, OP.is_equal, ["z1"], ["ih"], 1024.0, OP.mult)
    ts(T.bm[:, :], T.z1[:, :], 0.0, OP.is_equal, ["z1"], ["bm"])
    ts(T.dm[:, 0:32, 4], T.z1[:, 3::4], 0.0, OP.mult, ["z1"], ["dm2"])
    ts(T.dm[:, 32:64, 4], T.z1[:, 3::4], 0.0, OP.is_equal, ["z1"], ["dm3"], 20.0, OP.mult)
    tt(T.f01[0:80, :], T.fs[0:80, 0:256], T.fs[0:80, 256:512], OP.add, ["fs00", "fs01", "fs10", "fs11"], ["f01"])
    act(T.ident[:, :], T.ib[:, :], ["ib"], ["ident"])
    tt(T.f23[0:80, :], T.fs[0:80, 512:768], T.fs[0:80, 768:1024], OP.add, ["fs20", "fs21", "fs30", "fs31"], ["f23"])
    ts(T.ge[:, :], T.z4[:, :], 0.0, OP.is_ge, ["z4"], ["ge"])
    vcopy(T.tb[0:80, :], T.ti[0:80, :], ["tiw", "tib"], ["tb"])
    tt(T.f01[0:80, :], T.f01[0:80, :], T.f23[0:80, :], OP.add, ["f23"], ["f01"])
    tt(T.tm2[:, :], T.tmp[:, :], T.ib[:, :], OP.subtract, ["tmp", "ib"], ["tm2"])

    def cols(b):
        return slice(512 * b, 512 * b + 512)

    for b, bank in enumerate(("R0", "R1", "D0", "X0", "X1", "K0", "K1", "D1")):
        h, a = divmod(b, 4)
        for s in range(4):
            mm(T[bank][:, s::4], T.fs[0:80, 256 * s + 128 * h:256 * s + 128 * h + 128], T.tb[0:80, a::4], True, True,
               ["fs%d%d" % (s, h), "tb"], ["stg%s%d" % (bank, s)], [bank])
        if b % 3 == 1:
            ts(T.wsb[:, cols(b)], T[bank][:, :], 1.0 / 1024, OP.mult, four("stg" + bank), ["ws%d" % b], banks=[bank])
        else:
            act(T.wsb[:, cols(b)], T[bank][:, :], four("stg" + bank), ["ws%d" % b], [bank], scale=1.0 / 1024)

    def list_half(h):
        ts(T.lf[:, 128 * h:128 * h + 128], T.off[:, 128 * h:128 * h + 128], -2048.0, OP.add, ["off%d" % h], ["lf%d" % h])

    ts(T.fw[0:80, :], T.f01[0:80, :], -1.0, OP.mult, ["f01"], ["fw"])
    ts(T.dm[:, 0:32, 0:4], T.tm2[:, :], 7.0, OP.mult, ["tm2"], ["dm0"])
    ts(T.dm[:, 32:64, 0:4], T.tm2[:, :], 13.0, OP.mult, ["tm2"], ["dm1"])
    tt(T.bk[:, 0:8], T.ge[:, 1:9], T.ge[:, 0:8], OP.subtract, ["ge"], ["bk0"])
    tt(T.bk[:, 8:16], T.ge[:, 0:8], T.ge[:, 1:9], OP.subtract, ["ge"], ["bk1"])
    tt(T.bk[:, 16:17], T.ge[:, 0:1], T.ge[:, 1:2], OP.subtract, ["ge"], ["bk2"])
    vcopy(T.svm[:, 0:7], T.bk[:, 1:8], ["bk0"], ["svm0"])
    vcopy(T.svm[:, 7:8], T.bk[:, 0:1], ["bk0"], ["svm1"])
    for h in range(2):
        vcopy(T.off[:, 128 * h:128 * h + 128], T.lraw[:, :, h, :], four("lraw"), ["off%d" % h])
    list_half(0)
    list_half(1)

    def gathered(r, b):
        return T["win%d" % r][:, 0:4096].indirect(T.off[:, 32 * b:32 * b + 32])

    def win_keys(r, b):
        return ["arr%d" % r, "v%d0" % r, "v%d1" % r, "off%d" % (b // 4)]

    def gather(r, b):
        if b in FUSED[r]:
            act(T.p[:, cols(b)], gathered(r, b), win_keys(r, b), ["p%d" % b])
        else:
            act(T.p[:, cols(b)], gathered(r, b), win_keys(r, b), ["p%d" % b], (), AF.Identity, 1.0, 1.0)

    def gather_weigh(r, b):
        tt(T.wp[:, cols(b)], gathered(r, b), T.wsb[:, cols(b)], OP.mult, win_keys(r, b) + ["ws%d" % b], ["wp%d" % b])

    def weigh(r, b):
        op("V", lambda: V.tensor_tensor_scan(T.wp[:, cols(b)], T.p[:, cols(b)], T.wsb[:, cols(b)], 0.0, OP.max, OP.mult),
           ["p%d" % b, "ws%d" % b], ["wp%d" % b])

    def bias(r, h):
        X = T["X%d" % h]
        mm(X[:, :], T.fb[0:80, 128 * h:128 * h + 128], T.tb[0:80, :], True, False, ["fb%d" % h, "tb"], ["xb%d" % h, "xv%d" % h], ["X%d" % h])
        for a in range(4):
            if 4 * h + a not in FUSED[r]:
                mm(X[:, a::4], T.fw[0:80, 128 * h:128 * h + 128], T.tb[0:80, a::4], False, False, ["fw"], ["xb%d" % h], ["X%d" % h])

    done = {}

    def closes(key):
        done[key] = done.get(key, 0) + 1
        return done[key] == 4

    def wsum(r, b):
        h, a = divmod(b, 4)
        last = closes(("x", r, h))
        for s in range(4):
            mm(T["X%d" % h][:, a::4], T.ih[:, :], T.wp[:, 512 * b + s:512 * b + 512:4], False, last and s == 3,
               ["ih", "wp%d" % b, "xb%d" % h], ["x%d%d" % (h, a)], ["X%d" % h])

    def diffs(r, h):
        mm(T["D%d" % h][:, 0:320], T.lf[:, 128 * h:128 * h + 128], T.dm[:, :, :], True, False, ["lf%d" % h] + four("dm"), ["d%d" % h], ["D%d" % h])

    def keys_open(r, h):
        K = T["K%d" % h]
        mm(K[:, 0:400], T.ones[0:1, :], T.koff[0:1, :], True, False, ["ones", "koff4"] + four("koff"),
           ["kb%d" % h, "ks%d" % h] + four("k%d" % h), ["K%d" % h])
        mm(K[:, 272:400], T.lf[:, 128 * h:128 * h + 128], T.bm[:, :], False, False, ["lf%d" % h, "bm"], ["ks%d" % h], ["K%d" % h])

    def new_act(r, h):
        return (T.vo, 512 * h) if r == RO - 1 else (T["win%d" % (r + 1)], R + 512 * h)

    def clamp(r, h):
        buf, c0 = new_act(r, h)
        key = "v%d%d" % (r + 1, h)
        ts(buf[:, c0:c0 + 512], T["X%d" % h][:, :], 0.0, OP.max, four("x%d" % h), [key], 255.0, OP.min, ["X%d" % h])
        pass_on(r, h, key)

    def clamp_scalar(r, h):
        buf, c0 = new_act(r, h)
        key = "v%d%d" % (r + 1, h)
        act(T.yb[:, cols(h)], T["X%d" % h][:, :], four("x%d" % h) + ["c255"], ["yb%d" % h], ["X%d" % h], AF.Relu, T.c255[:, 0:1], -1.0)
        act(buf[:, c0:c0 + 512], T.yb[:, cols(h)], ["yb%d" % h], [key], (), AF.Relu, T.c255[:, 0:1], -1.0)
        pass_on(r, h, key)

    def pass_on(r, h, key):
        if r == RO - 1:
            dma("Y", T.ya[:, 512 * h:512 * h + 512], T.vo[:, 512 * h:512 * h + 512], "st", 96, rd=[key])
        else:
            send(r + 1, h)

    def act_to_psum(r, h):
        buf, c0 = new_act(r, h)
        for a in range(4):
            mm(T["X%d" % h][:, 128 * a:128 * a + 128], T.ib[:, :], buf[:, c0 + a:c0 + 512:4], True, True,
               ["ib", "v%d%d" % (r + 1, h)], ["xv%d" % h], ["X%d" % h])

    def act_sums(r, h):
        buf, c0 = new_act(r, h)
        for a in range(4):
            for cc in range(4):
                if 4 * h + a not in FUSED[r]:
                    mm(T["D%d" % h][32 * a:32 * a + 32, 164 + 5 * cc:320:20], buf[:, c0 + 4 * cc + a:c0 + 512:16], T.svm[:, :], False, False,
                       ["svm0", "svm1", "v%d%d" % (r + 1, h)], ["d%d" % h], ["D%d" % h])

    def prod(r, h, s, a0=0, a1=4):
        c = 2048 * h + 512 * s
        tt(T.pv[:, c + 128 * a0:c + 128 * a1], T.p[:, 2048 * h + 512 * a0 + s:2048 * h + 512 * a1:4], T["X%d" % h][:, 128 * a0:128 * a1],
           OP.mult, ["p%d" % (4 * h + a) for a in range(a0, a1)] + ["xv%d" % h], ["pv%d%d%d" % (h, s, a) for a in range(a0, a1)], ["X%d" % h])

    def score(r, h, s):
        c = 2048 * h + 512 * s
        last = closes(("k", r, h))
        for cc in range(4):
            mm(T["K%d" % h][:, 4 * cc + s:272:16], T.pv[:, c + cc:c + 512:4], T.bk[:, 0:17], False, last and cc == 3,
               four("pv%d%d" % (h, s)) + ["bk0", "bk1", "bk2", "kb%d" % h], ["k%d%d" % (h, s)], ["K%d" % h])

    def scan1(r, h):
        op("V", lambda: V.tensor_tensor_scan(T["mx%d" % h][:, :], T.rst[:, :], T["K%d" % h][:, 0:272], 0.0, OP.add, OP.max),
           ["rst"] + four("k%d" % h), ["mx%d" % h], ["K%d" % h])

    def flags(r, h):
        K, mx = T["K%d" % h], T["mx%d" % h]
        for s in range(4):
            tt(T["ne%d" % h][:, s::5], K[:, s:256:4], mx[:, 3:256:4], OP.not_equal, ["k%d%d" % (h, s), "mx%d" % h, "one%d" % h],
               ["ne%d%d" % (h, s)], ["K%d" % h])

    def worst_scalar(r, h):
        act(T["ew%d" % h][:, :], T["ne%d" % h][:, 0:160], four("ne%d" % h), ["ew%d" % h], (), AF.Identity, 1.0, -1.0)

    def worst(r, h):
        ts(T["ew%d" % h][:, :], T["ne%d" % h][:, 0:160], -1.0, OP.mult, four("ne%d" % h), ["ew%d" % h], 1.0, OP.add)

    def scan2(r, h):
        op("V", lambda: V.tensor_tensor_scan(T["yy%d" % h][:, :], T["D%d" % h][:, 0:320], T["ne%d" % h][:, :], 0.0, OP.add, OP.mult),
           ["d%d" % h] + four("ne%d" % h), ["yy%d" % h], ["D%d" % h])

    def base(r, h):
        mm(T["D%d" % h][:, 164:320:5], T.ident[:, :], T["mx%d" % h][:, 147:272:4], False, True, ["mx%d" % h, "ident"], ["d%d" % h], ["D%d" % h])

    def kept(r, h):
        K = T["K%d" % h]
        for s in range(4):
            tt(T["sk%d" % h][:, s::4], T["ne%d" % h][:, s:160:5], K[:, 272 + s:400:4], OP.mult, ["ne%d%d" % (h, s), "ks%d" % h],
               ["sk%d%d" % (h, s)], ["K%d" % h])
        mm(K[:, 272:400], T["sk%d" % h][:, :], T.ident[:, :], True, False, four("sk%d" % h) + ["ident"], ["ks%d" % h], ["K%d" % h])

    def to_int(r, h):
        yy = T["yy%d" % h]
        tt(T["ai%d" % h][:, 0:32], yy[:, 4:160:5], yy[:, 164:320:5], OP.add, ["yy%d" % h], ["a3%d" % h])

    def modulo(r, h):
        ai = T["ai%d" % h]
        ts(ai[:, 32:64], ai[:, 0:32], 4095, OP.bitwise_and, ["a3%d" % h], ["a4%d" % h])

    def rewire(r, h):
        for s in range(4):
            tt(T["tt%d" % h][:, s::4], T["ew%d" % h][:, s::5], T["ai%d" % h][:, 32:64], OP.mult, ["ew%d" % h, "a4%d" % h], ["tt%d%d" % (h, s)])
        mm(T["K%d" % h][:, 272:400], T["tt%d" % h][:, :], T.ident[:, :], False, True, four("tt%d" % h), ["ks%d" % h], ["K%d" % h])

    def offsets(r, h):
        out, key = (T.off[:, 128 * h:128 * h + 128], "off%d" % h) if r < RO - 1 else (T.ly[:, :, h, :], "ly%d" % h)
        vcopy(out, T["K%d" % h][:, 272:400], ["ks%d" % h], [key], ["K%d" % h])

    def list_step(r, h):
        if r < RO - 1:
            list_half(h)

    STEP = {"B": bias, "D": diffs, "K": keys_open, "F": gather_weigh, "G": gather, "W": weigh, "X": wsum, "C": clamp, "c": clamp_scalar,
            "A": act_to_psum, "V": act_sums, "M": prod, "S": score, "T": scan1, "N": flags, "E": worst_scalar, "e": worst, "Q": base, "H": kept,
            "Y": scan2, "I": to_int, "J": modulo, "Z": rewire, "O": offsets, "L": list_step}
    for r in range(RO):
        for step in ORDERS[r]:
            STEP[step[0]](r - step.count("'"), *[int(c) for c in step[1:].strip("'")])
    for a in range(4):
        dma("YS"[a % 2], T.ys[a::4, :], T.ly[:, a, :, :], "st", 96, rd=["ly0", "ly1"])
    need("G", [("V", cnt["V"]), ("S", cnt["S"]), ("P", cnt["P"]), ("G", cnt["G"]), ("sent", sent[0]), ("hand0", hand0), ("hand1", handed[0] - hand0), ("st", 96)])
